import numpy as np, ml_dtypes
CORES = [23,119,17,113]
N = 4
import mx_ref
BF = ml_dtypes.bfloat16
def f(rng, *shape):
    return mx_ref.flush((rng.standard_normal(shape, dtype=np.float32) * np.exp2(rng.integers(-2, 3, shape[:-1] + (1,)))).astype(BF))
def wide(rng, *shape, cols=0):
    v = rng.standard_normal(shape, dtype=np.float32) * np.exp2(rng.integers(-12, 13, shape)).astype(np.float32)
    if cols: v *= np.repeat(np.exp2(rng.integers(-cols, cols + 1, shape[:-2] + (1, shape[-1] // 4))) * (rng.random(shape[:-2] + (1, shape[-1] // 4)) > 0.0625), 4, axis=-1).astype(np.float32)
    return mx_ref.flush(v.astype(BF))
def cols(t, e):
    v = np.concatenate([t.reshape(128, -1, 4), np.zeros((128, 1, 4), BF)], axis=1)
    return np.ascontiguousarray(v[:, e]).reshape(128, -1)
def tile(rs):
    return np.stack(rs, axis=2).reshape(128, -1).astype(BF)
def cut(t, i, w=512):
    return t[:, w * i:w * i + w]
def decode(q):
    o = []
    for b in range(4):
        e = np.zeros((128, 128, 4), np.float32); e[np.arange(128), np.arange(128), b] = 1
        o.append(mx_ref.matmul(mx_ref.quantize(e.reshape(128, 512).astype(BF)), q))
    return np.stack(o, axis=2).reshape(128, -1)
T, CK = 512, 192
def gates(g):
    t = np.zeros((128, 512), BF); t[:, :4 * N] = g
    return np.stack([t] * N)
def plus(g):
    return np.maximum(np.abs(g.astype(np.float32)), np.float32(0.0625)).astype(BF)
def apart(rng):
    g = np.zeros((128, 4 * N), BF)
    for e in range(N): g[8 * e:8 * e + 8, 4 * e:4 * e + 4] = plus(f(rng, 8, 4))
    return g
def setup_inputs(rng):
    return {"x": f(rng, N, 128, 4 * T), "wg": gates(f(rng, 128, 4 * N)), "w1": f(rng, N, 128, 2048)}
def setup_inputs_alike(rng):
    d = setup_inputs(rng); d["wg"] = gates(np.tile(f(rng, 128, 4), (1, N))); return d
def setup_inputs_ties(rng):
    d = setup_inputs(rng); d["wg"] = gates(plus(f(rng, 128, 4 * N))); d["x"] = -plus(d["x"])
    for s in range(N):
        k = rng.permutation(np.arange(T) // 5 if s % 2 else np.arange(T) % (T // (CK + 1)))
        d["x"][s] = d["x"][s].reshape(128, T, 4)[:, k].reshape(128, -1)
    return d
def setup_inputs_split(rng):
    d = setup_inputs(rng); g = apart(rng)
    v = d["x"].astype(np.float32).reshape(N, 128, T, 4)
    for s in range(N):
        p = rng.permutation(T)
        for e in range(N):
            sign = np.full((1, T, 1), -1, np.float32); sign[:, p[(e * CK + np.arange(CK)) % T]] = 1
            v[s, 8 * e:8 * e + 8] = np.abs(v[s, 8 * e:8 * e + 8]) * sign
    d["x"] = v.reshape(N, 128, 4 * T).astype(BF); d["wg"] = gates(g); return d
def setup_inputs_zeros(rng):
    d = setup_inputs(rng); g = apart(rng)
    v = d["x"].astype(np.float32).reshape(N, 128, T, 4)
    for s in range(N):
        for e in range(N):
            p = rng.permutation(T); u = np.abs(v[s, 8 * e:8 * e + 8])
            u[:, p[CK // 2:CK // 2 + CK]] = np.where(rng.random((8, CK, 4)) < 0.5, np.float32(-0.0), np.float32(0.0))
            u[:, p[CK // 2 + CK:]] *= np.float32(-1)
            v[s, 8 * e:8 * e + 8] = u
    d["x"] = v.reshape(N, 128, 4 * T).astype(BF); d["wg"] = gates(g); return d
def setup_inputs_spread(rng):
    d = setup_inputs(rng); d["x"] = wide(rng, N, 128, 4 * T, cols=6); return d
def check_inputs(d):
    b = []
    g = d["wg"].astype(np.float32)
    if (g != g[0]).any() or (g[:, :, 4 * N:] != 0).any(): b.append("wg")
    return b
def reference(x, wg, w1):
    took = []
    for s in range(N):
        z = mx_ref.matmul(mx_ref.quantize(wg[s]), mx_ref.quantize(x[s])) + np.float32(0.0)
        took.append([np.argsort(-z[e], kind="stable")[:CK] for e in range(N)])
    y = np.zeros((N, 128, T, 4), np.float32)
    for e in range(N):
        q = mx_ref.quantize(np.concatenate([cols(x[s], took[s][e]) for s in range(N)], axis=1))
        rs = [np.maximum(mx_ref.matmul(mx_ref.quantize(np.ascontiguousarray(cut(w1[e], i))), q), np.float32(0.0)) * np.float32(0.05) for i in range(4)]
        v = decode(mx_ref.quantize(tile(rs))).reshape(128, N, CK, 4)
        for s in range(N): y[s][:, took[s][e]] += v[:, s]
    return {"y": y.reshape(N, 128, 4 * T)}

@@ -1,0 +1,401 @@
+from concourse.mybir import dt, AluOpType, AxisListType, ActivationFunctionType
+
+A = AluOpType
+F = ActivationFunctionType
+NR, CK = 4, 192
+NS = 9
+NV = 16 - NS
+CS = 2
+CV = 6 - CS
+PW = 8 + NR * CK
+XP = ((0, 256), (256, 384), (384, 512))
+YP = ((0, 64), (64, 160), (160, 320), (320, 512))
+BIG = 1e29
+
+SCRATCH = {
+    "xs": ("sbuf", [128, 2048], "bfloat16"), "xs1": ("sbuf", [128, 2064], "bfloat16"),
+    "xs2": ("sbuf", [128, 2064], "bfloat16"), "xs3": ("sbuf", [128, 2064], "bfloat16"),
+    "ws1": ("sbuf", [128, 2048], "bfloat16"),
+    "gs": ("sbuf", [128, 16], "bfloat16"), "gl1": ("sbuf", [128, 512], "bfloat16"),
+    "xq": ("sbuf", [128, 512], "float8_e4m3fn_x4"), "xc": ("sbuf", [128, 512], "uint8"),
+    "wq": ("sbuf", [128, 512], "float8_e4m3fn_x4"), "wc": ("sbuf", [128, 512], "uint8"),
+    "eq": ("sbuf", [128, 512], "float8_e4m3fn_x4"), "ec": ("sbuf", [128, 512], "uint8"),
+    "g1q": ("sbuf", [128, 128], "float8_e4m3fn_x4"), "g1c": ("sbuf", [128, 128], "uint8"),
+    "sq": ("sbuf", [128, 768], "float8_e4m3fn_x4"), "sc": ("sbuf", [128, 768], "uint8"),
+    "rq": ("sbuf", [128, 576], "float8_e4m3fn_x4"), "rc": ("sbuf", [128, 576], "uint8"),
+    "oq": ("sbuf", [128, 768], "float8_e4m3fn_x4"), "oc": ("sbuf", [128, 768], "uint8"),
+    "bq": ("sbuf", [128, 768], "float8_e4m3fn_x4"), "bc": ("sbuf", [128, 768], "uint8"),
+    "ones": ("sbuf", [128, 512], "bfloat16"), "zero": ("sbuf", [128, 512], "bfloat16"),
+    "zf": ("sbuf", [128, 32], "float32"), "et": ("sbuf", [128, 2048], "bfloat16"),
+    "ip": ("sbuf", [128, 64], "int32"), "ic": ("sbuf", [128, 64], "int32"),
+    "pa": ("sbuf", [128, 64], "int32"), "v": ("sbuf", [128, 64], "int32"), "t2": ("sbuf", [128, 32], "int32"),
+    "a1": ("sbuf", [128, 32], "int32"), "l1": ("sbuf", [128, 32], "int32"), "o1": ("sbuf", [128, 32], "uint16"),
+    "a2": ("sbuf", [128, 32], "int32"), "a3": ("sbuf", [128, 32], "int32"), "a4": ("sbuf", [128, 32], "int32"),
+    "ph": ("sbuf", [128, 8], "int32"), "pr": ("sbuf", [128, 8], "int32"), "pe": ("sbuf", [128, 8], "int32"),
+    "k0": ("sbuf", [128, 8], "int32"), "k1": ("sbuf", [128, 8], "int32"), "k2": ("sbuf", [128, 8], "int32"),
+    "kf": ("sbuf", [128, 8], "float32"), "kh": ("sbuf", [128, 8], "float32"), "base": ("sbuf", [128, 8], "float32"),
+    "u1": ("sbuf", [128, 32], "int32"), "u2": ("sbuf", [128, 32], "int32"), "u3": ("sbuf", [128, 32], "int32"),
+    "u4": ("sbuf", [128, 32], "int32"), "oT": ("sbuf", [128, 32], "uint16"),
+    "d0": ("sbuf", [128, 36], "float32"), "d1": ("sbuf", [128, 36], "int32"), "d2": ("sbuf", [128, 36], "int32"),
+    "d3": ("sbuf", [128, 36], "int32"), "d4": ("sbuf", [128, 36], "int32"), "oX": ("sbuf", [128, 36], "uint16"),
+    "zT": ("sbuf", [128, 512], "float32"), "junk": ("sbuf", [128, 512 * NS], "bfloat16"),
+    "accS": ("sbuf", [128, NS], "float32"),
+    "cmp": ("sbuf", [128, 512 * NV], "bfloat16"), "scv": ("sbuf", [128, 256 * NV], "bfloat16"),
+    "ma": ("sbuf", [128, 16], "float32"), "mb": ("sbuf", [128, 16], "float32"),
+    "za": ("sbuf", [128, 16], "float32"), "zb": ("sbuf", [128, 16], "float32"),
+    "ra": ("sbuf", [128, 1], "float32"), "rb": ("sbuf", [128, 1], "float32"),
+    "ex": ("sbuf", [128, 64], "float32"), "exT": ("sbuf", [128, 64], "float32"),
+    "va": ("sbuf", [128, 1], "float32"), "vb": ("sbuf", [128, 1], "float32"), "n2": ("sbuf", [128, 1], "float32"),
+    "sgA": ("sbuf", [128, 512], "bfloat16"), "sgB": ("sbuf", [128, 512], "bfloat16"),
+    "gea": ("sbuf", [128, 512], "bfloat16"), "sca": ("sbuf", [128, 256], "bfloat16"),
+    "gt": ("sbuf", [128, 512], "bfloat16"), "scg": ("sbuf", [128, 256], "bfloat16"), "geb": ("sbuf", [128, 512], "bfloat16"),
+    "dd": ("sbuf", [128, 512], "bfloat16"), "dd2": ("sbuf", [128, 512], "bfloat16"), "cb": ("sbuf", [128, 528], "bfloat16"),
+    "jk2": ("sbuf", [128, 512 * CS], "bfloat16"), "acc2": ("sbuf", [128, CS], "float32"),
+    "cm2": ("sbuf", [128, 512 * CV], "bfloat16"), "sc2": ("sbuf", [128, 256 * CV], "bfloat16"),
+    "tokc": ("sbuf", [128, 6], "uint16"), "tokw": ("sbuf", [128, 48], "uint16"), "tokr": ("sbuf", [128, 48], "uint16"),
+    "h": ("sbuf", [128, 3072], "bfloat16"), "rt": ("sbuf", [128, 3072], "bfloat16"),
+    "cx": ("sbuf", [128, 512], "float32"), "tk": ("sbuf", [128, 512], "bfloat16"),
+    "mf": ("sbuf", [128, 512], "float32"), "mt": ("sbuf", [128, 512], "float32"),
+    "xl": ("sbuf", [128, 576], "float32"), "xp": ("sbuf", [128, 576], "float32"),
+    "wt": ("sbuf", [128, 128], "float32"), "wsl": ("sbuf", [128, 108], "float32"),
+    "lt1": ("sbuf", [128, 64], "float32"), "lt2": ("sbuf", [128, 32], "float32"), "oL": ("sbuf", [128, 32], "uint16"),
+    "sl": ("sbuf", [128, 36], "float32"), "m3": ("sbuf", [128, 12], "float32"), "oS": ("sbuf", [128, 36], "uint16"),
+    "G": ("sbuf", [128, 2304], "float32"), "P": ("sbuf", [128, 4 * PW], "float32"),
+    "ys": ("sbuf", [128, 2048], "float32"),
+}
+for _b in range(8):
+    SCRATCH["ps%d" % _b] = ("psum", [128, 512], "float32")
+SEMAPHORES = ["cv", "cs", "ct", "cg", "lx0", "lx1", "lx2", "lh1", "lh2", "lh3", "lg", "lw", "wr0", "wr1", "wr2", "wr3",
+              "lwt", "lws", "sty", "sent", "rd0", "rd1", "rd2", "rd3", "rr0", "rr1", "rr2", "rr3"]
+
+
+def rank_program(g, core, T, topo):
+    me = T.rank_of(core)
+    if me is None:
+        return
+    S = T.sem
+    Q = {"v": g.vector, "s": g.scalar, "t": g.tensor, "g": g, "y": g.sync}
+    cnt, waited, tot = {}, {}, {}
+
+    def need(q, deps):
+        best = {}
+        for sem, val in deps:
+            best[sem] = max(val, best.get(sem, 0))
+        for sem, val in best.items():
+            if waited.get((q, sem), 0) < val:
+                Q[q].wait_ge(S[sem], val)
+                waited[(q, sem)] = val
+
+    def done(q, ins):
+        cnt[q] = cnt.get(q, 0) + 1
+        ins.then_inc(S["c" + q], 1)
+        return ("c" + q, cnt[q])
+
+    def ts(out, in0, s1, op0, s2=None, op1=None, deps=()):
+        need("v", deps)
+        if op1 is None:
+            return done("v", g.vector.tensor_scalar(out, in0, s1, None, op0))
+        return done("v", g.vector.tensor_scalar(out, in0, s1, s2, op0, op1))
+
+    def tt(out, a, b, op, deps=()):
+        need("v", deps)
+        return done("v", g.vector.tensor_tensor(out, a, b, op))
+
+    def cp(out, a, deps=()):
+        need("v", deps)
+        return done("v", g.vector.tensor_copy(out, a))
+
+    def ms(out, c):
+        return done("v", g.vector.memset(out, c))
+
+    def red(out, a, op, deps=()):
+        need("v", deps)
+        return done("v", g.vector.tensor_reduce(out, a, AxisListType.X, op))
+
+    def scan(out, a, b, init, op0, op1, deps=()):
+        need("v", deps)
+        return done("v", g.vector.tensor_tensor_scan(out, a, b, init, op0, op1))
+
+    def tr(out, a, deps=()):
+        need("v", deps)
+        return done("v", g.vector.transpose(out, a))
+
+    def quant(out, sc, a, deps=()):
+        need("v", deps)
+        return done("v", g.vector.quantize_mx(out, sc, a))
+
+    def act(out, a, func, deps=(), **kw):
+        need("s", deps)
+        return done("s", g.scalar.activation(out, a, func, **kw))
+
+    def mm(out, l, ls, r, rs, deps=()):
+        need("t", deps)
+        return done("t", g.tensor.matmul_mx(out, l, ls, r, rs, True, True))
+
+    def dma(q, sem, out, in_, deps=()):
+        need(q, deps)
+        Q[q].dma_start(out, in_).then_inc(S[sem], 16)
+        tot[sem] = tot.get(sem, 0) + 16
+        return (sem, tot[sem])
+
+    def order(r):
+        c = T.cores[r]
+        near = [k for k in range(NR) if topo.chip(T.cores[k]) == topo.chip(c)]
+        off = [k for k in range(NR) if k not in near]
+        i = near.index(r)
+        return [off[i], off[1 - i]] + [k for k in near if k != r] + [r]
+    O = order(me)
+    SLOT = (0, 3, 2, 1)
+    E = [1, 0, 2, 3] if 1 in O[2:] else [0, 1, 2, 3]
+    B = [E.index(r) for r in O]
+    eoff = topo.engines(core, T.cores[O[0]])
+    eon = [e for e in topo.engines(core, T.cores[O[2]]) if e not in eoff] or eoff
+    part = {O[0]: eoff, O[1]: eoff, O[2]: eon}
+
+    def mask(es):
+        return sum(1 << e for e in es)
+
+    lg = dma("s", "lg", T.gs[:], T.wg[:, 0:16])
+    lx = [dma("y", "lx%d" % i, T.xs[:, 4 * a:4 * b], T.x[:, 4 * a:4 * b]) for i, (a, b) in enumerate(XP)]
+    need("y", lx)
+    lsh = {0: lx}
+    for t in (2, 1, 3):
+        lsh[t] = [dma("y", "lh%d" % t, T["xs%d" % t][:, 16 - t:2064 - t], T.x[:])]
+    lw = dma("y", "lw", T.ws1[:], T.w1[:])
+
+    ip = done("g", g.iota(T.ip[:], [[0, 64]], 0, 1))
+    ic = done("g", g.iota(T.ic[:], [[16, 64]], 0, 0))
+    on1 = ms(T.ones[:], 1.0)
+    d = ts(T.pa[:], T.ip[:], 15, A.bitwise_and, deps=[ip])
+    v = tt(T.v[:], T.pa[:], T.ic[:], A.add, [d, ic])
+    t2 = ts(T.t2[:], T.v[:, 0:32], 3, A.bitwise_and, deps=[v])
+    a1 = ts(T.a1[:], T.v[:, 0:32], 5, A.arith_shift_right, 12, A.bitwise_and, [v])
+    if E[0] == 1:
+        a2 = ts(T.a2[:], T.a1[:], 8, A.is_lt, deps=[a1])
+        a3 = ts(T.a3[:], T.a1[:], -2, A.mult, 4, A.add, [a1])
+        a4 = tt(T.a4[:], T.a2[:], T.a3[:], A.mult, [a2, a3])
+        a1 = tt(T.a1[:], T.a1[:], T.a4[:], A.add, [a4])
+    l1 = tt(T.l1[:], T.a1[:], T.t2[:], A.add, [a1, t2])
+    o1 = cp(T.o1[:], T.l1[:], [l1])
+    zr = ms(T.zero[:], 0.0)
+    zf = ms(T.zf[:], 0.0)
+    cbz = ms(T.cb[:, 0:16], 0.0)
+    for b in range(4):
+        pz = ms(T.P[:, PW * b:PW * b + 8], 0.0)
+    et = []
+    for b in range(4):
+        need("g", [on1])
+        et.append(done("g", g.affine_select(T.et[:, 512 * b:512 * b + 512], T.ones[:], [[1, 512]], A.is_equal, 0.0, -b, -4)))
+
+    ph = ts(T.ph[:], T.ip[:, 0:8], 1, A.bitwise_and)
+    pr = ts(T.pr[:], T.ip[:, 0:8], 1, A.arith_shift_right, 15, A.bitwise_and)
+    pe = ts(T.pe[:], T.ip[:, 0:8], 5, A.arith_shift_right)
+    k0 = ts(T.k0[:], T.ph[:], 96, A.mult, deps=[ph])
+    bs = ts(T.base[:], T.pe[:], 192, A.mult, 7, A.add, [pe])
+    k1 = tt(T.k1[:], T.k0[:], T.pr[:], A.add, [k0, pr])
+    u1 = ts(T.u1[:], T.v[:, 0:32], 31, A.bitwise_and)
+    u2 = ts(T.u2[:], T.v[:, 0:32], 5, A.arith_shift_right)
+    d0 = ts(T.d0[:], T.v[:, 0:36], 1.0 / 36, A.mult, 0.5 / 36 - 0.5, A.add)
+    d3 = ts(T.d3[:], T.v[:, 0:36], 16, A.mult)
+    k2 = tt(T.k2[:], T.k1[:], T.ic[:, 0:8], A.add, [k1])
+    u3 = ts(T.u3[:], T.u1[:], 16, A.mult, deps=[u1])
+    d1 = cp(T.d1[:], T.d0[:], [d0])
+    kf = cp(T.kf[:], T.k2[:], [k2])
+    u4 = tt(T.u4[:], T.u3[:], T.u2[:], A.add, [u3, u2])
+    d2 = ts(T.d2[:], T.d1[:], -575, A.mult, deps=[d1])
+    kh = ts(T.kh[:], T.kf[:], 0.5, A.add, deps=[kf])
+    oT = cp(T.oT[:], T.u4[:], [u4])
+    d4 = tt(T.d4[:], T.d3[:], T.d2[:], A.add, [d3, d2])
+    oX = cp(T.oX[:], T.d4[:], [d4])
+
+    g1 = act(T.gl1[:], T.gs[:, 0:16].indirect(T.o1[:, 0:32]), F.Copy, [lg, o1])
+    g1 = quant(T.g1q[:], T.g1c[:], T.gl1[:], [g1])
+
+    xq = [quant(T.xq[:, a:b], T.xc[:, a:b], T.xs[:, 4 * a:4 * b], [lx[i]]) for i, (a, b) in enumerate(XP)]
+    zV = mm(T.ps0[:], T.g1q[:], T.g1c[:], T.xq[:], T.xc[:], [g1] + xq)
+    zS = mm(T.ps1[:], T.g1q[:], T.g1c[:], T.xq[:], T.xc[:])
+    zt0 = tr(T.zT[:, 0:64], T.ps0[:, 0:64], [zV])
+    zt1 = tr(T.zT[:, 64:512], T.ps0[:, 64:512])
+    for c in range(NS):
+        aS = act(T.junk[:, 512 * c:512 * c + 512], T.ps1[:], F.Sign, [zS, zt0 if c < 2 else zt1],
+                 bias=T.zT[:, 32 * c:32 * c + 1], scale=-1.0, accum_out=T.accS[:, c:c + 1])
+    prev = None
+    for i in range(NV + 1):
+        if i < NV:
+            c = NS + i
+            cur = ts(T.cmp[:, 512 * i:512 * i + 512], T.ps0[:], T.zT[:, 32 * c:32 * c + 1], A.is_gt, deps=[zt1])
+        if i > 0:
+            k = i - 1
+            wV = scan(T.scv[:, 256 * k:256 * k + 256], T.cmp[:, 512 * k:512 * k + 256], T.cmp[:, 512 * k + 256:512 * k + 512],
+                      -191.5, A.add, A.add, [prev])
+        prev = cur
+    b2 = ts(T.ma[:, NS:16], T.scv[:, 255:256 * NV:256], 0.0, A.is_gt, BIG, A.mult, [wV])
+    b4 = ts(T.mb[:, NS:16], T.scv[:, 255:256 * NV:256], 0.0, A.is_lt, -BIG, A.mult)
+    b1 = ts(T.ma[:, 0:NS], T.accS[:], 128.0, A.is_lt, BIG, A.mult, [aS])
+    b3 = ts(T.mb[:, 0:NS], T.accS[:], 128.0, A.is_ge, -BIG, A.mult)
+    za = tt(T.za[:], T.zT[:, 0:512:32], T.ma[:], A.add, [b1, b2])
+    zb = tt(T.zb[:], T.zT[:, 0:512:32], T.mb[:], A.add, [b3, b4])
+    ra = red(T.ra[:], T.za[:], A.min, [za])
+    rb = red(T.rb[:], T.zb[:], A.max, [zb])
+    xa = ts(T.ex[:, 0:32], T.zf[:], T.ra[:], A.add, deps=[ra, zf])
+    xb = ts(T.ex[:, 32:64], T.zf[:], T.rb[:], A.add, deps=[rb])
+    xt = tr(T.exT[:], T.ex[:], [xa, xb])
+    va = red(T.va[:], T.exT[:, 0:32], A.min, [xt])
+    vb = red(T.vb[:], T.exT[:, 32:64], A.max)
+    sA = act(T.sgA[:], T.ps1[:], F.Sign, [va], bias=T.va[:], scale=-1.0)
+    sB = act(T.sgB[:], T.ps1[:], F.Sign, [vb], bias=T.vb[:], scale=-1.0)
+    ga = ts(T.gea[:], T.ps0[:], T.va[:], A.is_ge, deps=[va])
+    sa = scan(T.sca[:], T.gea[:, 0:256], T.gea[:, 256:512], -192.0, A.add, A.add, [ga])
+    gt = ts(T.gt[:], T.sgA[:], 0.0, A.is_lt, -1.0, A.mult, [sA])
+    n2 = ts(T.n2[:], T.sca[:, 255:256], -1.0, A.mult, 0.0, A.max, [sa])
+    n1 = scan(T.scg[:], T.gt[:, 0:256], T.gt[:, 256:512], 192.0, A.add, A.add, [gt])
+    d1 = scan(T.dd[:], T.zero[:], T.gt[:], T.scg[:, 255:256], A.add, A.subtract, [n1, zr])
+    gb = ts(T.geb[:], T.sgB[:], 0.0, A.is_le, deps=[sB])
+    d2 = scan(T.dd2[:], T.gea[:], T.dd[:], T.n2[:], A.add, A.min, [d1, n2])
+    C = scan(T.cb[:, 16:528], T.geb[:], T.dd2[:], 0.0, A.add, A.min, [d2, gb])
+    for c in range(CS):
+        aS = act(T.jk2[:, 512 * c:512 * c + 512], T.cb[:, 16:528], F.Sign, [C, kh],
+                 bias=T.kh[:, c:c + 1], scale=-1.0, accum_out=T.acc2[:, c:c + 1])
+    for i in range(CV + 1):
+        if i < CV:
+            cur = ts(T.cm2[:, 512 * i:512 * i + 512], T.cb[:, 16:528], T.kf[:, CS + i:CS + i + 1], A.is_le, deps=[C, kf])
+        if i > 0:
+            k = i - 1
+            wV = scan(T.sc2[:, 256 * k:256 * k + 256], T.cm2[:, 512 * k:512 * k + 256], T.cm2[:, 512 * k + 256:512 * k + 512],
+                      -256.0, A.add, A.add, [prev])
+        prev = cur
+    tc0 = ts(T.tokc[:, 0:CS], T.acc2[:], 2.0, A.mult, 1024.0, A.add, [aS])
+    tc1 = ts(T.tokc[:, CS:6], T.sc2[:, 255:256 * CV:256], 4.0, A.mult, 1024.0, A.add, [wV])
+    wr = []
+    for o in range(NR):
+        for i in range(8):
+            w = dma("ys"[i % 2], "wr%d" % o, T.tokw[16 * i:16 * i + 16, 12 * o:12 * o + 12],
+                    T.tokc[32 * B[o]:32 * B[o] + 32, :], [tc0, tc1])
+        wr.append(w)
+    cx = act(T.cx[:], T.cb[:, 16:528], F.Identity, [C, bs], bias=T.base[:, 0:1])
+    wq = quant(T.wq[:], T.wc[:], T.ws1[:], [lw])
+    tk = tt(T.tk[:], T.cb[:, 16:528], T.cb[:, 15:527], A.subtract, [C, cbz])
+
+    def gather(o):
+        r = []
+        for t in range(4):
+            out = T.h[:, 768 * o + t:768 * o + 768:4]
+            win = T.xs[:, 0:2048] if t == 0 else T["xs%d" % t][:, 16:2064 - t]
+            src = win.indirect(T.tokw[:, 12 * o:12 * o + 12])
+            dep = [wr[o]] + lsh[t]
+            r.append(cp(out, src, dep) if t < 2 else act(out, src, F.Copy, dep))
+        return quant(T.sq[:, CK * o:CK * o + CK], T.sc[:, CK * o:CK * o + CK], T.h[:, 768 * o:768 * o + 768], r)
+
+    def send(o, sb, sp, db, dp, sem, dep):
+        r = O[o]
+        p = order(r).index(me)
+        if sem == "rr":
+            p = SLOT[p]
+        rid, pid, _ = topo.addr(T.cores[r])
+        need("g", [dep])
+        for a, b, code in ((sb, db, True), (sp, dp, False)):
+            src, dst = T[a][:, CK * o:CK * o + CK], T[b][:, CK * p:CK * p + CK]
+            if code:
+                src, dst = src.bitcast(dt.uint8), dst.bitcast(dt.uint8)
+            g.remote_dma(out_ap=dst, in_ap=src, remote_sem=S["%s%d" % (sem, me)], local_sem=S["sent"], pid=pid,
+                         routing_id=rid, dma_engine_mask=mask(part[r]))
+            tot["sent"] = tot.get("sent", 0) + len(part[r])
+
+    def arrived(sem, o):
+        return (sem + str(O[o]), 2 * len(part[O[o]]))
+
+    for o in range(3):
+        send(o, "sq", "sc", "rq", "rc", "rd", gather(o))
+    qown = gather(3)
+    mf = tt(T.mf[:], T.cx[:], T.tk[:], A.mult, [cx, tk])
+    tr4 = ts(T.tokr[:], T.tokw[:], 0.25, A.mult, deps=wr)
+
+    free = [[sA, sB, C], []]
+
+    def expert(bset, cq, cc, o, qout, qsc, z, deps):
+        rd, m = [], {}
+        for i in (0, 2, 1, 3):
+            m[i] = mm(T["ps%d" % (4 * bset + i)][:, 0:CK], T.wq[:, 128 * i:128 * i + 128], T.wc[:, 128 * i:128 * i + 128],
+                      T[cq][:, CK * o:CK * o + CK], T[cc][:, CK * o:CK * o + CK], list(deps) + [wq] + free[bset])
+        for i in range(4):
+            out = T.rt[:, 768 * o + i:768 * o + 768:4]
+            src = T["ps%d" % (4 * bset + i)][:, 0:CK]
+            if i < 2:
+                rd.append(ts(out, src, 0.0, A.max, 0.05, A.mult, [m[i]]))
+            else:
+                rd.append(act(out, src, F.Relu, [m[i]], scale=0.05))
+        free[bset] = rd
+        return quant(T[qout][:, CK * z:CK * z + CK], T[qsc][:, CK * z:CK * z + CK], T.rt[:, 768 * o:768 * o + 768], rd)
+
+    q3 = expert(1, "sq", "sc", 3, "bq", "bc", SLOT[3], [qown])
+    eqd = quant(T.eq[:], T.ec[:], T.et[:], et)
+    mt = cp(T.mt[:], T.mf[:].indirect(T.oT[:]), [mf, oT])
+    for q in range(1, NR):
+        c0 = 12 * B.index(q)
+        xl = act(T.xl[:, CK * (q - 1):CK * q], T.mf[:].indirect(T.tokr[:, c0:c0 + 12]), F.Copy, [mf, tr4])
+    xp = act(T.xp[:], T.xl[:].indirect(T.oX[:]), F.Copy, [xl, oX])
+    for q in range(NR):
+        lt = dma("y", "lwt", T.wt[:, 32 * q:32 * q + 32], T.mt[32 * q:32 * q + 8, :], [mt])
+    for q in range(NR - 1):
+        ls = dma("y", "lws", T.wsl[:, 36 * q:36 * q + 36], T.xp[32 * q:32 * q + 8, :], [xp])
+    for bset, o in ((0, 0), (1, 2), (0, 1)):
+        send(o, "oq", "oc", "bq", "bc", "rr", expert(bset, "rq", "rc", o, "oq", "oc", o, [arrived("rd", o)]))
+
+    x = tt(T.lt1[:], T.wt[:, 0:64], T.wt[:, 64:128], A.max, [lt])
+    s0 = cp(T.sl[:, 0:12], T.wsl[:, 0:12], [ls])
+    s1 = tt(T.sl[:, 12:24], T.wsl[:, 12:24], T.wsl[:, 48:60], A.max)
+    s2 = tt(T.m3[:], T.wsl[:, 24:36], T.wsl[:, 60:72], A.max)
+    x = tt(T.lt2[:], T.lt1[:, 0:32], T.lt1[:, 32:64], A.max, [x])
+    s2 = tt(T.sl[:, 24:36], T.m3[:], T.wsl[:, 96:108], A.max, [s2])
+    oL = cp(T.oL[:], T.lt2[:], [x])
+    oS = cp(T.oS[:], T.sl[:], [s0, s1, s2])
+
+    dm, got, gs = {}, {}, {}
+
+    def decode(bset, z, blocks, deps):
+        n = len(blocks) * CK
+        for b in range(4):
+            m = mm(T["ps%d" % (4 * bset + b)][:, 0:n], T.eq[:, 128 * b:128 * b + 128], T.ec[:, 128 * b:128 * b + 128],
+                   T.bq[:, CK * z:CK * z + n], T.bc[:, CK * z:CK * z + n], deps[b] + [eqd])
+            for i, q in enumerate(blocks):
+                dm[(q, b)] = (m, T["ps%d" % (4 * bset + b)][:, CK * i:CK * i + CK])
+
+    own = B[3] == 0
+    decode(0, 0, [B[0], B[3]] if own else [B[0]], [[arrived("rr", 0), q3] + free[0]] * 4)
+    decode(1, 2, [B[2]], [[arrived("rr", 2)] + free[1]] * 4)
+
+    def first(b):
+        m, src = dm[(0, b)]
+        out = T.P[:, PW * b + 8:PW * b + 8 + CK]
+        got[b] = cp(out, src, [m]) if b % 2 == 0 else act(out, src, F.Copy, [m])
+
+    def pick(q, b):
+        out = T.G[:, 768 * (q - 1) + CK * b:768 * (q - 1) + CK * b + CK]
+        src = T.P[:, PW * b:PW * b + 8 + CK * q].indirect(T.oS[:, 12 * (q - 1):12 * q])
+        dep = [got[b], oS, pz]
+        gs[b] = (cp(out, src, dep) if b == 0 else act(out, src, F.Copy, dep), out)
+
+    def add(q, b):
+        m, src = dm[(q, b)]
+        got[b] = tt(T.P[:, PW * b + 8 + CK * q:PW * b + 8 + CK * (q + 1)], src, gs[b][1], A.add, [m, gs[b][0], got[b]])
+
+    for b in range(4):
+        first(b)
+    for q in range(1, NR):
+        if q == (2 if own else 1):
+            decode(0 if own else 1, 3, [B[1]], [[arrived("rr", 1), got[b]] for b in range(4)])
+        if q == B[3]:
+            decode(0 if B[0] == q - 1 else 1, 1, [q], [[got[b]] for b in range(4)])
+        for b in range(4):
+            pick(q, b)
+        for b in range(4):
+            add(q, b)
+    for a, z in YP:
+        r = []
+        for b in range(4):
+            out = T.ys[:, 4 * a + b:4 * z:4]
+            src = T.P[:, PW * b:PW * b + PW].indirect(T.oL[:, a // 16:z // 16])
+            dep = [got[b], oL]
+            r.append(cp(out, src, dep) if b < 2 else act(out, src, F.Copy, dep))
+        st = dma("y", "sty", T.y[:, 4 * a:4 * z], T.ys[:, 4 * a:4 * z], r)
+    need("y", [(k, n) for k, n in tot.items()] + [("c" + k, n) for k, n in cnt.items()])

@@ -2,15 +2,18 @@ from concourse.mybir import dt, AluOpType, AxisListType, ActivationFunctionType
 
 A = AluOpType
 F = ActivationFunctionType
-NR, CK = 4, 192
+NR, CK, NT = 4, 192, 512
 NS = 9
 NV = 16 - NS
-CS = 2
-CV = 6 - CS
+CV = 4
+CS = 6 - CV
+WV = NT - CK + 32
+WS = NT - 32 * CV
 PW = 8 + NR * CK
 XP = ((0, 256), (256, 384), (384, 512))
 YP = ((0, 64), (64, 160), (160, 320), (320, 512))
-BIG = 1e29
+BIG = 1e26
+FB = 3
 
 SCRATCH = {
     "xs": ("sbuf", [128, 2048], "bfloat16"), "xs1": ("sbuf", [128, 2064], "bfloat16"),
@@ -25,48 +28,34 @@ SCRATCH = {
     "rq": ("sbuf", [128, 576], "float8_e4m3fn_x4"), "rc": ("sbuf", [128, 576], "uint8"),
     "oq": ("sbuf", [128, 768], "float8_e4m3fn_x4"), "oc": ("sbuf", [128, 768], "uint8"),
     "bq": ("sbuf", [128, 768], "float8_e4m3fn_x4"), "bc": ("sbuf", [128, 768], "uint8"),
-    "ones": ("sbuf", [128, 512], "bfloat16"), "zero": ("sbuf", [128, 512], "bfloat16"),
-    "zf": ("sbuf", [128, 32], "float32"), "et": ("sbuf", [128, 2048], "bfloat16"),
-    "ip": ("sbuf", [128, 64], "int32"), "ic": ("sbuf", [128, 64], "int32"),
-    "pa": ("sbuf", [128, 64], "int32"), "v": ("sbuf", [128, 64], "int32"), "t2": ("sbuf", [128, 32], "int32"),
-    "a1": ("sbuf", [128, 32], "int32"), "l1": ("sbuf", [128, 32], "int32"), "o1": ("sbuf", [128, 32], "uint16"),
-    "a2": ("sbuf", [128, 32], "int32"), "a3": ("sbuf", [128, 32], "int32"), "a4": ("sbuf", [128, 32], "int32"),
-    "ph": ("sbuf", [128, 8], "int32"), "pr": ("sbuf", [128, 8], "int32"), "pe": ("sbuf", [128, 8], "int32"),
-    "k0": ("sbuf", [128, 8], "int32"), "k1": ("sbuf", [128, 8], "int32"), "k2": ("sbuf", [128, 8], "int32"),
-    "kf": ("sbuf", [128, 8], "float32"), "kh": ("sbuf", [128, 8], "float32"), "base": ("sbuf", [128, 8], "float32"),
-    "u1": ("sbuf", [128, 32], "int32"), "u2": ("sbuf", [128, 32], "int32"), "u3": ("sbuf", [128, 32], "int32"),
-    "u4": ("sbuf", [128, 32], "int32"), "oT": ("sbuf", [128, 32], "uint16"),
-    "d0": ("sbuf", [128, 36], "float32"), "d1": ("sbuf", [128, 36], "int32"), "d2": ("sbuf", [128, 36], "int32"),
-    "d3": ("sbuf", [128, 36], "int32"), "d4": ("sbuf", [128, 36], "int32"), "oX": ("sbuf", [128, 36], "uint16"),
+    "ones": ("sbuf", [128, 512], "bfloat16"), "et": ("sbuf", [128, 2048], "bfloat16"),
+    "ip": ("sbuf", [128, 32], "int32"), "ic": ("sbuf", [128, 32], "int32"),
+    "t2": ("sbuf", [128, 32], "int32"), "l1": ("sbuf", [128, 32], "int32"), "o1": ("sbuf", [128, 32], "uint16"),
+    "k2": ("sbuf", [128, 8], "float32"), "base": ("sbuf", [128, 8], "float32"),
     "zT": ("sbuf", [128, 512], "float32"), "junk": ("sbuf", [128, 512 * NS], "bfloat16"),
     "accS": ("sbuf", [128, NS], "float32"),
     "cmp": ("sbuf", [128, 512 * NV], "bfloat16"), "scv": ("sbuf", [128, 256 * NV], "bfloat16"),
-    "ma": ("sbuf", [128, 16], "float32"), "mb": ("sbuf", [128, 16], "float32"),
-    "za": ("sbuf", [128, 16], "float32"), "zb": ("sbuf", [128, 16], "float32"),
-    "ra": ("sbuf", [128, 1], "float32"), "rb": ("sbuf", [128, 1], "float32"),
-    "ex": ("sbuf", [128, 64], "float32"), "exT": ("sbuf", [128, 64], "float32"),
-    "va": ("sbuf", [128, 1], "float32"), "vb": ("sbuf", [128, 1], "float32"), "n2": ("sbuf", [128, 1], "float32"),
-    "sgA": ("sbuf", [128, 512], "bfloat16"), "sgB": ("sbuf", [128, 512], "bfloat16"),
-    "gea": ("sbuf", [128, 512], "bfloat16"), "sca": ("sbuf", [128, 256], "bfloat16"),
-    "gt": ("sbuf", [128, 512], "bfloat16"), "scg": ("sbuf", [128, 256], "bfloat16"), "geb": ("sbuf", [128, 512], "bfloat16"),
-    "dd": ("sbuf", [128, 512], "bfloat16"), "dd2": ("sbuf", [128, 512], "bfloat16"), "cb": ("sbuf", [128, 528], "bfloat16"),
-    "jk2": ("sbuf", [128, 512 * CS], "bfloat16"), "acc2": ("sbuf", [128, CS], "float32"),
-    "cm2": ("sbuf", [128, 512 * CV], "bfloat16"), "sc2": ("sbuf", [128, 256 * CV], "bfloat16"),
-    "tokc": ("sbuf", [128, 6], "uint16"), "tokw": ("sbuf", [128, 48], "uint16"), "tokr": ("sbuf", [128, 48], "uint16"),
+    "mk": ("sbuf", [128, 16], "float32"), "za": ("sbuf", [128, 48], "float32"), "zb": ("sbuf", [128, 48], "float32"),
+    "sg": ("sbuf", [128, 16], "float32"), "rn": ("sbuf", [128, 1], "float32"), "nb": ("sbuf", [128, 1], "float32"),
+    "ex": ("sbuf", [128, 128], "float32"), "exT": ("sbuf", [128, 96], "float32"),
+    "ns": ("sbuf", [128, 1], "float32"), "vs": ("sbuf", [128, 32], "float32"),
+    "sgA": ("sbuf", [128, 512], "bfloat16"), "ge": ("sbuf", [128, 512], "bfloat16"),
+    "gt": ("sbuf", [128, 512], "bfloat16"), "dd": ("sbuf", [128, 512], "bfloat16"), "cb": ("sbuf", [128, 528], "bfloat16"),
+    "jk2": ("sbuf", [128, WS * CS], "bfloat16"), "acc2": ("sbuf", [128, CS], "float32"),
+    "cm2": ("sbuf", [128, WV * CV], "bfloat16"), "sc2": ("sbuf", [128, WV // 2 * CV], "bfloat16"),
+    "X0": ("sbuf", [128, 64], "float32"), "Z0": ("sbuf", [128, 64], "float32"), "W0": ("sbuf", [128, 64], "float32"),
+    "Z1": ("sbuf", [128, 64], "float32"), "W1": ("sbuf", [128, 64], "float32"),
+    "tokw": ("sbuf", [128, 48], "uint16"), "tokr": ("sbuf", [128, 48], "uint16"),
     "h": ("sbuf", [128, 3072], "bfloat16"), "rt": ("sbuf", [128, 3072], "bfloat16"),
-    "cx": ("sbuf", [128, 512], "float32"), "tk": ("sbuf", [128, 512], "bfloat16"),
-    "mf": ("sbuf", [128, 512], "float32"), "mt": ("sbuf", [128, 512], "float32"),
-    "xl": ("sbuf", [128, 576], "float32"), "xp": ("sbuf", [128, 576], "float32"),
-    "wt": ("sbuf", [128, 128], "float32"), "wsl": ("sbuf", [128, 108], "float32"),
-    "lt1": ("sbuf", [128, 64], "float32"), "lt2": ("sbuf", [128, 32], "float32"), "oL": ("sbuf", [128, 32], "uint16"),
-    "sl": ("sbuf", [128, 36], "float32"), "m3": ("sbuf", [128, 12], "float32"), "oS": ("sbuf", [128, 36], "uint16"),
-    "G": ("sbuf", [128, 2304], "float32"), "P": ("sbuf", [128, 4 * PW], "float32"),
+    "tk": ("sbuf", [128, 512], "bfloat16"), "mr": ("sbuf", [128, 1088], "bfloat16"), "mT": ("sbuf", [128, 1088], "bfloat16"),
+    "pu": ("sbuf", [128, 34], "float32"), "pos": ("sbuf", [128, 34], "float32"), "oL": ("sbuf", [128, 68], "uint16"),
+    "G": ("sbuf", [128, 2304], "float32"), "P": ("sbuf", [128, 4 * PW], "float32"), "D": ("sbuf", [128, 768], "float32"),
     "ys": ("sbuf", [128, 2048], "float32"),
 }
 for _b in range(8):
     SCRATCH["ps%d" % _b] = ("psum", [128, 512], "float32")
-SEMAPHORES = ["cv", "cs", "ct", "cg", "lx0", "lx1", "lx2", "lh1", "lh2", "lh3", "lg", "lw", "wr0", "wr1", "wr2", "wr3",
-              "lwt", "lws", "sty", "sent", "rd0", "rd1", "rd2", "rd3", "rr0", "rr1", "rr2", "rr3"]
+SEMAPHORES = ["cv", "cs", "ct", "cg", "lx0", "lx1", "lx2", "lh1", "lh2", "lh3", "lg", "lw",
+              "sty", "sent", "rd0", "rd1", "rd2", "rd3", "rr0", "rr1", "rr2", "rr3"]
 
 
 def rank_program(g, core, T, topo):
@@ -138,6 +127,16 @@ def rank_program(g, core, T, topo):
         tot[sem] = tot.get(sem, 0) + 16
         return (sem, tot[sem])
 
+    def iota(out, pattern, base, cm):
+        need("g", [("cg", cnt["g"])])
+        return done("g", g.iota(out, pattern, base, cm, allow_small_or_imprecise_dtypes=True))
+
+    def move(on, out, a, deps):
+        return cp(out, a, deps) if on == "v" else act(out, a, F.Copy, deps)
+
+    def quad(t, e, a, b, step=1):
+        return t[32 * e:32 * e + 32, a:b:step]
+
     def order(r):
         c = T.cores[r]
         near = [k for k in range(NR) if topo.chip(T.cores[k]) == topo.chip(c)]
@@ -158,55 +157,31 @@ def rank_program(g, core, T, topo):
     lg = dma("s", "lg", T.gs[:], T.wg[:, 0:16])
     lx = [dma("y", "lx%d" % i, T.xs[:, 4 * a:4 * b], T.x[:, 4 * a:4 * b]) for i, (a, b) in enumerate(XP)]
     need("y", lx)
+    lw = dma("y", "lw", T.ws1[:], T.w1[:])
     lsh = {0: lx}
     for t in (2, 1, 3):
         lsh[t] = [dma("y", "lh%d" % t, T["xs%d" % t][:, 16 - t:2064 - t], T.x[:])]
-    lw = dma("y", "lw", T.ws1[:], T.w1[:])
 
-    ip = done("g", g.iota(T.ip[:], [[0, 64]], 0, 1))
-    ic = done("g", g.iota(T.ic[:], [[16, 64]], 0, 0))
+    ip = done("g", g.iota(T.ip[:], [[0, 32]], 0, 1))
+    ic = done("g", g.iota(T.ic[:], [[4, 4], [0, 8]], 0, 0))
     on1 = ms(T.ones[:], 1.0)
-    d = ts(T.pa[:], T.ip[:], 15, A.bitwise_and, deps=[ip])
-    v = tt(T.v[:], T.pa[:], T.ic[:], A.add, [d, ic])
-    t2 = ts(T.t2[:], T.v[:, 0:32], 3, A.bitwise_and, deps=[v])
-    a1 = ts(T.a1[:], T.v[:, 0:32], 5, A.arith_shift_right, 12, A.bitwise_and, [v])
-    if E[0] == 1:
-        a2 = ts(T.a2[:], T.a1[:], 8, A.is_lt, deps=[a1])
-        a3 = ts(T.a3[:], T.a1[:], -2, A.mult, 4, A.add, [a1])
-        a4 = tt(T.a4[:], T.a2[:], T.a3[:], A.mult, [a2, a3])
-        a1 = tt(T.a1[:], T.a1[:], T.a4[:], A.add, [a4])
-    l1 = tt(T.l1[:], T.a1[:], T.t2[:], A.add, [a1, t2])
+    t2 = ts(T.t2[:], T.ip[:], 3, A.bitwise_and, deps=[ip])
+    ms(T.za[:, 16:48], BIG)
+    l1 = tt(T.l1[:], T.ic[:], T.t2[:], A.add, [ic, t2])
+    ms(T.zb[:, 16:48], -BIG)
     o1 = cp(T.o1[:], T.l1[:], [l1])
-    zr = ms(T.zero[:], 0.0)
-    zf = ms(T.zf[:], 0.0)
-    cbz = ms(T.cb[:, 0:16], 0.0)
-    for b in range(4):
-        pz = ms(T.P[:, PW * b:PW * b + 8], 0.0)
+    ms(T.cb[:, 0:16], 0.0)
+    ms(T.dd[:, 511:512], float(CK))
+    ms(T.X0[:], 0.0)
+    ms(T.nb[:], (NT - 2 * CK + 1) / 32 * BIG)
+    pz = ms(T.P[:, 0:4 * PW:PW], 0.0)
+    for e in range(NR):
+        iota(quad(T.k2, e, 0, 8), [[64, 8]], 1, 2)
+        kb = iota(quad(T.base, e, 0, 8), [[0, 8]], CK * E.index(e), 0)
     et = []
     for b in range(4):
-        need("g", [on1])
+        need("g", [on1, kb])
         et.append(done("g", g.affine_select(T.et[:, 512 * b:512 * b + 512], T.ones[:], [[1, 512]], A.is_equal, 0.0, -b, -4)))
-
-    ph = ts(T.ph[:], T.ip[:, 0:8], 1, A.bitwise_and)
-    pr = ts(T.pr[:], T.ip[:, 0:8], 1, A.arith_shift_right, 15, A.bitwise_and)
-    pe = ts(T.pe[:], T.ip[:, 0:8], 5, A.arith_shift_right)
-    k0 = ts(T.k0[:], T.ph[:], 96, A.mult, deps=[ph])
-    bs = ts(T.base[:], T.pe[:], 192, A.mult, 7, A.add, [pe])
-    k1 = tt(T.k1[:], T.k0[:], T.pr[:], A.add, [k0, pr])
-    u1 = ts(T.u1[:], T.v[:, 0:32], 31, A.bitwise_and)
-    u2 = ts(T.u2[:], T.v[:, 0:32], 5, A.arith_shift_right)
-    d0 = ts(T.d0[:], T.v[:, 0:36], 1.0 / 36, A.mult, 0.5 / 36 - 0.5, A.add)
-    d3 = ts(T.d3[:], T.v[:, 0:36], 16, A.mult)
-    k2 = tt(T.k2[:], T.k1[:], T.ic[:, 0:8], A.add, [k1])
-    u3 = ts(T.u3[:], T.u1[:], 16, A.mult, deps=[u1])
-    d1 = cp(T.d1[:], T.d0[:], [d0])
-    kf = cp(T.kf[:], T.k2[:], [k2])
-    u4 = tt(T.u4[:], T.u3[:], T.u2[:], A.add, [u3, u2])
-    d2 = ts(T.d2[:], T.d1[:], -575, A.mult, deps=[d1])
-    kh = ts(T.kh[:], T.kf[:], 0.5, A.add, deps=[kf])
-    oT = cp(T.oT[:], T.u4[:], [u4])
-    d4 = tt(T.d4[:], T.d3[:], T.d2[:], A.add, [d3, d2])
-    oX = cp(T.oX[:], T.d4[:], [d4])
 
     g1 = act(T.gl1[:], T.gs[:, 0:16].indirect(T.o1[:, 0:32]), F.Copy, [lg, o1])
     g1 = quant(T.g1q[:], T.g1c[:], T.gl1[:], [g1])
@@ -227,63 +202,62 @@ def rank_program(g, core, T, topo):
         if i > 0:
             k = i - 1
             wV = scan(T.scv[:, 256 * k:256 * k + 256], T.cmp[:, 512 * k:512 * k + 256], T.cmp[:, 512 * k + 256:512 * k + 512],
-                      -191.5, A.add, A.add, [prev])
+                      0.5 - CK, A.add, A.add, [prev])
         prev = cur
-    b2 = ts(T.ma[:, NS:16], T.scv[:, 255:256 * NV:256], 0.0, A.is_gt, BIG, A.mult, [wV])
-    b4 = ts(T.mb[:, NS:16], T.scv[:, 255:256 * NV:256], 0.0, A.is_lt, -BIG, A.mult)
-    b1 = ts(T.ma[:, 0:NS], T.accS[:], 128.0, A.is_lt, BIG, A.mult, [aS])
-    b3 = ts(T.mb[:, 0:NS], T.accS[:], 128.0, A.is_ge, -BIG, A.mult)
-    za = tt(T.za[:], T.zT[:, 0:512:32], T.ma[:], A.add, [b1, b2])
-    zb = tt(T.zb[:], T.zT[:, 0:512:32], T.mb[:], A.add, [b3, b4])
-    ra = red(T.ra[:], T.za[:], A.min, [za])
-    rb = red(T.rb[:], T.zb[:], A.max, [zb])
-    xa = ts(T.ex[:, 0:32], T.zf[:], T.ra[:], A.add, deps=[ra, zf])
-    xb = ts(T.ex[:, 32:64], T.zf[:], T.rb[:], A.add, deps=[rb])
-    xt = tr(T.exT[:], T.ex[:], [xa, xb])
-    va = red(T.va[:], T.exT[:, 0:32], A.min, [xt])
-    vb = red(T.vb[:], T.exT[:, 32:64], A.max)
-    sA = act(T.sgA[:], T.ps1[:], F.Sign, [va], bias=T.va[:], scale=-1.0)
-    sB = act(T.sgB[:], T.ps1[:], F.Sign, [vb], bias=T.vb[:], scale=-1.0)
-    ga = ts(T.gea[:], T.ps0[:], T.va[:], A.is_ge, deps=[va])
-    sa = scan(T.sca[:], T.gea[:, 0:256], T.gea[:, 256:512], -192.0, A.add, A.add, [ga])
+    m1 = ts(T.mk[:, NS:16], T.scv[:, 255:256 * NV:256], BIG, A.mult, deps=[wV])
+    m0 = ts(T.mk[:, 0:NS], T.accS[:], NT - 2 * CK - 0.5, A.subtract, -BIG, A.mult, [aS])
+    za = tt(T.za[:, 0:16], T.zT[:, 0:512:32], T.mk[:], A.max, [m0, m1])
+    zb = tt(T.zb[:, 0:16], T.zT[:, 0:512:32], T.mk[:], A.min)
+    rn = act(T.sg[:], T.mk[:], F.Sign, [m0, m1], accum_out=T.rn[:])
+    xn = act(T.ex[:, 48:80], T.zb[:, 16:48], F.Identity, [rn], scale=T.rn[:], bias=T.nb[:])
+    xa = scan(T.ex[:, 0:48], T.za[:], T.za[:], BIG, A.min, A.min, [za])
+    xb = scan(T.ex[:, 127:79:-1], T.zb[:], T.zb[:], -BIG, A.max, A.max, [zb])
+    xt = tr(T.exT[:], T.ex[:, 16:112], [xa, xb, xn])
+    ns = red(T.ns[:], T.exT[:, 32:64], A.add, [xt])
+    vs = scan(T.vs[:], T.exT[:, 0:32], T.exT[:, 64:96], T.ns[:], A.min, A.max, [ns])
+    sA = act(T.sgA[:], T.ps1[:], F.Sign, [vs], bias=T.vs[:, 31:32], scale=-1.0)
+    ge = ts(T.ge[:], T.ps0[:], T.vs[:, 31:32], A.is_ge, deps=[vs])
     gt = ts(T.gt[:], T.sgA[:], 0.0, A.is_lt, -1.0, A.mult, [sA])
-    n2 = ts(T.n2[:], T.sca[:, 255:256], -1.0, A.mult, 0.0, A.max, [sa])
-    n1 = scan(T.scg[:], T.gt[:, 0:256], T.gt[:, 256:512], 192.0, A.add, A.add, [gt])
-    d1 = scan(T.dd[:], T.zero[:], T.gt[:], T.scg[:, 255:256], A.add, A.subtract, [n1, zr])
-    gb = ts(T.geb[:], T.sgB[:], 0.0, A.is_le, deps=[sB])
-    d2 = scan(T.dd2[:], T.gea[:], T.dd[:], T.n2[:], A.add, A.min, [d1, n2])
-    C = scan(T.cb[:, 16:528], T.geb[:], T.dd2[:], 0.0, A.add, A.min, [d2, gb])
+    dd = scan(T.dd[:, 510::-1], T.gt[:, 511:0:-1], T.gt[:, 511:0:-1], float(CK), A.add, A.max, [gt])
+    C = scan(T.cb[:, 16:528], T.ge[:], T.dd[:], 0.0, A.add, A.min, [dd, ge])
     for c in range(CS):
-        aS = act(T.jk2[:, 512 * c:512 * c + 512], T.cb[:, 16:528], F.Sign, [C, kh],
-                 bias=T.kh[:, c:c + 1], scale=-1.0, accum_out=T.acc2[:, c:c + 1])
+        aS = act(T.jk2[:, WS * c:WS * c + WS], T.cb[:, 528 - WS:528], F.Sign, [C, kb],
+                 bias=T.k2[:, CV + c:CV + c + 1], scale=-2.0, accum_out=T.acc2[:, c:c + 1])
+    H = WV // 2
     for i in range(CV + 1):
         if i < CV:
-            cur = ts(T.cm2[:, 512 * i:512 * i + 512], T.cb[:, 16:528], T.kf[:, CS + i:CS + i + 1], A.is_le, deps=[C, kf])
+            cur = ts(T.cm2[:, WV * i:WV * i + WV], T.cb[:, 16 + 32 * i:16 + 32 * i + WV], 2.0, A.mult,
+                     T.k2[:, i:i + 1], A.is_lt, [C, kb])
         if i > 0:
             k = i - 1
-            wV = scan(T.sc2[:, 256 * k:256 * k + 256], T.cm2[:, 512 * k:512 * k + 256], T.cm2[:, 512 * k + 256:512 * k + 512],
-                      -256.0, A.add, A.add, [prev])
+            wV = scan(T.sc2[:, H * k:H * k + H], T.cm2[:, WV * k:WV * k + H], T.cm2[:, WV * k + H:WV * k + WV],
+                      32.0 * k - 256.0, A.add, A.add, [prev])
         prev = cur
-    tc0 = ts(T.tokc[:, 0:CS], T.acc2[:], 2.0, A.mult, 1024.0, A.add, [aS])
-    tc1 = ts(T.tokc[:, CS:6], T.sc2[:, 255:256 * CV:256], 4.0, A.mult, 1024.0, A.add, [wV])
-    wr = []
+    x0 = []
     for o in range(NR):
-        for i in range(8):
-            w = dma("ys"[i % 2], "wr%d" % o, T.tokw[16 * i:16 * i + 16, 12 * o:12 * o + 12],
-                    T.tokc[32 * B[o]:32 * B[o] + 32, :], [tc0, tc1])
-        wr.append(w)
-    cx = act(T.cx[:], T.cb[:, 16:528], F.Identity, [C, bs], bias=T.base[:, 0:1])
-    wq = quant(T.wq[:], T.wc[:], T.ws1[:], [lw])
-    tk = tt(T.tk[:], T.cb[:, 16:528], T.cb[:, 15:527], A.subtract, [C, cbz])
+        x0.append(act(T.X0[0:32, 6 * o + CV:6 * o + 6], quad(T.acc2, O[o], 0, CS), F.Identity, [aS, pz],
+                      scale=2.0, bias=4.0 * (NT - WS) + 2.0 * WS))
+    for o in range(NR):
+        out, src = T.X0[0:32, 6 * o:6 * o + CV], quad(T.sc2, O[o], H - 1, H * CV, H)
+        x0.append(ts(out, src, 4.0, A.mult, 1024.0, A.add, [wV]) if o % 2 == 0 else
+                  act(out, src, F.Identity, [wV], scale=4.0, bias=1024.0))
+
+    def wrap(n, W, Z, X, deps):
+        z = tr(Z[0:n, 16:48], X, deps)
+        d0 = cp(Z[0:n, 0:16], Z[0:n, 16:32], [z])
+        d1 = cp(Z[0:n, 48:64], Z[0:n, 32:48])
+        tr(W[0:n, 0:64:2], Z[0:n, 0:32], [d0])
+        return tr(W[0:n, 1:64:2], Z[0:n, 32:64], [d1])
+    w = wrap(32, T.W0, T.Z0, T.X0[0:32, 0:32], x0)
+    for a in range(4):
+        wr = cp(quad(T.tokw, a, 0, 48), T.W0[0:32, 0:48], [w])
 
     def gather(o):
         r = []
         for t in range(4):
             out = T.h[:, 768 * o + t:768 * o + 768:4]
             win = T.xs[:, 0:2048] if t == 0 else T["xs%d" % t][:, 16:2064 - t]
-            src = win.indirect(T.tokw[:, 12 * o:12 * o + 12])
-            dep = [wr[o]] + lsh[t]
-            r.append(cp(out, src, dep) if t < 2 else act(out, src, F.Copy, dep))
+            r.append(move("vvss"[t], out, win.indirect(T.tokw[:, 12 * o:12 * o + 12]), [wr] + lsh[t]))
         return quant(T.sq[:, CK * o:CK * o + CK], T.sc[:, CK * o:CK * o + CK], T.h[:, 768 * o:768 * o + 768], r)
 
     def send(o, sb, sp, db, dp, sem, dep):
@@ -306,15 +280,14 @@ def rank_program(g, core, T, topo):
 
     for o in range(3):
         send(o, "sq", "sc", "rq", "rc", "rd", gather(o))
+    wq = quant(T.wq[:], T.wc[:], T.ws1[:], [lw])
     qown = gather(3)
-    mf = tt(T.mf[:], T.cx[:], T.tk[:], A.mult, [cx, tk])
-    tr4 = ts(T.tokr[:], T.tokw[:], 0.25, A.mult, deps=wr)
 
-    free = [[sA, sB, C], []]
+    free = [[sA, ge], []]
 
     def expert(bset, cq, cc, o, qout, qsc, z, deps):
         rd, m = [], {}
-        for i in (0, 2, 1, 3):
+        for i in (2, 0, 3, 1):
             m[i] = mm(T["ps%d" % (4 * bset + i)][:, 0:CK], T.wq[:, 128 * i:128 * i + 128], T.wc[:, 128 * i:128 * i + 128],
                       T[cq][:, CK * o:CK * o + CK], T[cc][:, CK * o:CK * o + CK], list(deps) + [wq] + free[bset])
         for i in range(4):
@@ -327,30 +300,32 @@ def rank_program(g, core, T, topo):
         free[bset] = rd
         return quant(T[qout][:, CK * z:CK * z + CK], T[qsc][:, CK * z:CK * z + CK], T.rt[:, 768 * o:768 * o + 768], rd)
 
+    tr4 = ts(T.tokr[:], T.tokw[:], 0.25, A.mult, deps=[wr])
+    tk = tt(T.tk[:], T.cb[:, 16:528], T.cb[:, 15:527], A.subtract, [C])
     q3 = expert(1, "sq", "sc", 3, "bq", "bc", SLOT[3], [qown])
-    eqd = quant(T.eq[:], T.ec[:], T.et[:], et)
-    mt = cp(T.mt[:], T.mf[:].indirect(T.oT[:]), [mf, oT])
-    for q in range(1, NR):
-        c0 = 12 * B.index(q)
-        xl = act(T.xl[:, CK * (q - 1):CK * q], T.mf[:].indirect(T.tokr[:, c0:c0 + 12]), F.Copy, [mf, tr4])
-    xp = act(T.xp[:], T.xl[:].indirect(T.oX[:]), F.Copy, [xl, oX])
-    for q in range(NR):
-        lt = dma("y", "lwt", T.wt[:, 32 * q:32 * q + 32], T.mt[32 * q:32 * q + 8, :], [mt])
-    for q in range(NR - 1):
-        ls = dma("y", "lws", T.wsl[:, 36 * q:36 * q + 36], T.xp[32 * q:32 * q + 8, :], [xp])
+    mr = tt(T.mr[:, 0:512], T.cb[:, 16:528], T.tk[:], A.mult, [tk])
     for bset, o in ((0, 0), (1, 2), (0, 1)):
         send(o, "oq", "oc", "bq", "bc", "rr", expert(bset, "rq", "rc", o, "oq", "oc", o, [arrived("rd", o)]))
+    for i in range(3):
+        c0 = 12 * B.index(3 - i)
+        xl = act(T.mr[:, 512 + CK * i:512 + CK * (i + 1)], T.mr[:, 0:512].indirect(T.tokr[:, c0:c0 + 12]), F.Copy, [mr, tr4])
+    eqd = quant(T.eq[:], T.ec[:], T.et[:], et)
 
-    x = tt(T.lt1[:], T.wt[:, 0:64], T.wt[:, 64:128], A.max, [lt])
-    s0 = cp(T.sl[:, 0:12], T.wsl[:, 0:12], [ls])
-    s1 = tt(T.sl[:, 12:24], T.wsl[:, 12:24], T.wsl[:, 48:60], A.max)
-    s2 = tt(T.m3[:], T.wsl[:, 24:36], T.wsl[:, 60:72], A.max)
-    x = tt(T.lt2[:], T.lt1[:, 0:32], T.lt1[:, 32:64], A.max, [x])
-    s2 = tt(T.sl[:, 24:36], T.m3[:], T.wsl[:, 96:108], A.max, [s2])
-    oL = cp(T.oL[:], T.lt2[:], [x])
-    oS = cp(T.oS[:], T.sl[:], [s0, s1, s2])
+    tr(T.mT[:, 0:512], T.mr[:, 0:512], [mr])
+    x = tr(T.mT[:, 512:1088], T.mr[:, 512:1088], [xl])
+    x = ts(T.pu[:], T.mT[:, 0:1088:32], 1024.0, A.mult, T.base[:, 0:1], A.min, [x])
+    x = tt(T.pos[:], T.pu[:], T.mT[:, 0:1088:32], A.add, [x])
+    for q, n in ((1, 28), (2, 22)):
+        x = tt(quad(T.pos, E[0], 0, n), quad(T.pos, E[0], 0, n), quad(T.pos, E[q], 0, n), A.max, [x])
+    tt(T.X0[0:32, 32:48], quad(T.pos, E[0], 0, 16), quad(T.pos, E[3], 0, 16), A.max, [x])
+    x = cp(T.X0[32:64, 32:50], quad(T.pos, E[0], 16, 34))
+    x = wrap(64, T.W1, T.Z1, T.X0[0:64, 32:64], [x])
+    for a in range(2):
+        cp(quad(T.oL, a, 0, 32), T.W1[0:32, 0:32], [x])
+        y = cp(quad(T.oL, a, 32, 68), T.W1[32:64, 0:36])
+    oL = cp(T.oL[64:128, :], T.oL[0:64, :], [y])
 
-    dm, got, gs = {}, {}, {}
+    dm, got, gs, sb = {}, {}, {}, {}
 
     def decode(bset, z, blocks, deps):
         n = len(blocks) * CK
@@ -360,42 +335,62 @@ def rank_program(g, core, T, topo):
             for i, q in enumerate(blocks):
                 dm[(q, b)] = (m, T["ps%d" % (4 * bset + b)][:, CK * i:CK * i + CK])
 
-    own = B[3] == 0
-    decode(0, 0, [B[0], B[3]] if own else [B[0]], [[arrived("rr", 0), q3] + free[0]] * 4)
-    decode(1, 2, [B[2]], [[arrived("rr", 2)] + free[1]] * 4)
+    def slots(q, b):
+        return T.P[:, PW * b + 1 + CK * q:PW * b + 1 + CK * (q + 1)]
 
-    def first(b):
-        m, src = dm[(0, b)]
-        out = T.P[:, PW * b + 8:PW * b + 8 + CK]
-        got[b] = cp(out, src, [m]) if b % 2 == 0 else act(out, src, F.Copy, [m])
+    def earlier(q, b):
+        return T.P[:, PW * b:PW * b + 1 + CK * q].indirect(T.oL[:, 68 - 12 * q:80 - 12 * q])
 
-    def pick(q, b):
+    def first():
+        for b in range(4):
+            got[b] = move("svsv"[b], slots(0, b), dm[(0, b)][1], [dm[(0, b)][0]])
+
+    def pick(q, b, on):
         out = T.G[:, 768 * (q - 1) + CK * b:768 * (q - 1) + CK * b + CK]
-        src = T.P[:, PW * b:PW * b + 8 + CK * q].indirect(T.oS[:, 12 * (q - 1):12 * q])
-        dep = [got[b], oS, pz]
-        gs[b] = (cp(out, src, dep) if b == 0 else act(out, src, F.Copy, dep), out)
+        gs[b] = (move(on, out, earlier(q, b), [got[b], oL]), out)
 
     def add(q, b):
         m, src = dm[(q, b)]
-        got[b] = tt(T.P[:, PW * b + 8 + CK * q:PW * b + 8 + CK * (q + 1)], src, gs[b][1], A.add, [m, gs[b][0], got[b]])
+        got[b] = tt(slots(q, b), src, gs[b][1], A.add, [m, gs[b][0], got[b]])
 
-    for b in range(4):
-        first(b)
-    for q in range(1, NR):
-        if q == (2 if own else 1):
-            decode(0 if own else 1, 3, [B[1]], [[arrived("rr", 1), got[b]] for b in range(4)])
-        if q == B[3]:
-            decode(0 if B[0] == q - 1 else 1, 1, [q], [[got[b]] for b in range(4)])
+    def park(q):
+        sb[q] = act(T.D[:, CK * q:CK * q + CK], dm[(q, FB)][1], F.Copy, [dm[(q, FB)][0]])
+
+    def after(extra=()):
+        return [[got[b]] + list(extra) for b in range(4)]
+
+    last = B[1]
+    if B[3] == 0:
+        decode(0, 1, [0], [[q3] + free[0]] * 4)
+        first()
+        decode(0, 0, [1], after([arrived("rr", 0)]))
+        decode(1, 2, [B[2]], [[arrived("rr", 2)] + free[1]] * 4)
+        lastset = 0
+    else:
+        decode(0, 2, [0], [[arrived("rr", 2)] + free[0]] * 4)
+        first()
+        decode(0, 0, [B[0], B[3]], after([arrived("rr", 0), q3]))
+        lastset = 1
+    for q in range(1, last + 1):
         for b in range(4):
-            pick(q, b)
+            pick(q, b, "vsss"[b])
+        if q == last:
+            for p in range(last + 1, NR):
+                park(p)
+            decode(lastset, 3, [q], after([arrived("rr", 1)] + free[lastset]))
         for b in range(4):
+            add(q, b)
+    for q in range(last + 1, NR):
+        rest = [b for b in range(4) if b != FB]
+        for b in rest:
+            pick(q, b, "s")
+        got[FB] = tt(slots(q, FB), earlier(q, FB), T.D[:, CK * q:CK * q + CK], A.add, [got[FB], sb[q]])
+        for b in rest:
             add(q, b)
     for a, z in YP:
         r = []
-        for b in range(4):
-            out = T.ys[:, 4 * a + b:4 * z:4]
-            src = T.P[:, PW * b:PW * b + PW].indirect(T.oL[:, a // 16:z // 16])
-            dep = [got[b], oL]
-            r.append(cp(out, src, dep) if b < 2 else act(out, src, F.Copy, dep))
+        for b, on in ((FB, "s"), (0, "s"), (1, "v"), (2, "v")):
+            src = T.P[:, PW * b:PW * b + 1 + NR * CK].indirect(T.oL[:, a // 16:z // 16])
+            r.append(move(on, T.ys[:, 4 * a + b:4 * z:4], src, [got[b], oL]))
         st = dma("y", "sty", T.y[:, 4 * a:4 * z], T.ys[:, 4 * a:4 * z], r)
     need("y", [(k, n) for k, n in tot.items()] + [("c" + k, n) for k, n in cnt.items()])

@@ -5,6 +5,7 @@ F = ActivationFunctionType
 NR, CK, NT = 4, 192, 512
 NS = 9
 NV = 16 - NS
+ES, EV = 4, 3
 CV = 4
 CS = 6 - CV
 WV = NT - CK + 32
@@ -12,8 +13,14 @@ WS = NT - 32 * CV
 PW = 8 + NR * CK
 XP = ((0, 256), (256, 384), (384, 512))
 YP = ((0, 64), (64, 160), (160, 320), (320, 512))
-BIG = 1e26
-FB = 3
+GS = 352
+FI = 1
+F0 = (0, 1)
+OG = "vsss"
+FILL = (5, 0, 2, 99)
+LO = (0, 32, 68, 100, 132)
+BIG = 2.0 ** 86
+FB = (3, 2)
 
 SCRATCH = {
     "xs": ("sbuf", [128, 2048], "bfloat16"), "xs1": ("sbuf", [128, 2064], "bfloat16"),
@@ -28,15 +35,15 @@ SCRATCH = {
     "rq": ("sbuf", [128, 576], "float8_e4m3fn_x4"), "rc": ("sbuf", [128, 576], "uint8"),
     "oq": ("sbuf", [128, 768], "float8_e4m3fn_x4"), "oc": ("sbuf", [128, 768], "uint8"),
     "bq": ("sbuf", [128, 768], "float8_e4m3fn_x4"), "bc": ("sbuf", [128, 768], "uint8"),
-    "ones": ("sbuf", [128, 512], "bfloat16"), "et": ("sbuf", [128, 2048], "bfloat16"),
+    "ones": ("sbuf", [128, 128], "bfloat16"), "idn": ("sbuf", [128, 128], "bfloat16"), "et": ("sbuf", [128, 2048], "bfloat16"),
     "ip": ("sbuf", [128, 32], "int32"), "ic": ("sbuf", [128, 32], "int32"),
     "t2": ("sbuf", [128, 32], "int32"), "l1": ("sbuf", [128, 32], "int32"), "o1": ("sbuf", [128, 32], "uint16"),
     "k2": ("sbuf", [128, 8], "float32"), "base": ("sbuf", [128, 8], "float32"),
     "zT": ("sbuf", [128, 512], "float32"), "junk": ("sbuf", [128, 512 * NS], "bfloat16"),
-    "accS": ("sbuf", [128, NS], "float32"),
-    "cmp": ("sbuf", [128, 512 * NV], "bfloat16"), "scv": ("sbuf", [128, 256 * NV], "bfloat16"),
-    "mk": ("sbuf", [128, 16], "float32"), "za": ("sbuf", [128, 48], "float32"), "zb": ("sbuf", [128, 48], "float32"),
-    "sg": ("sbuf", [128, 16], "float32"), "rn": ("sbuf", [128, 1], "float32"), "nb": ("sbuf", [128, 1], "float32"),
+    "accS": ("sbuf", [128, NS + ES], "float32"),
+    "cmp": ("sbuf", [128, 512 * NV], "bfloat16"),
+    "mk": ("sbuf", [128, 272], "bfloat16"), "za": ("sbuf", [128, 48], "float32"), "zb": ("sbuf", [128, 48], "float32"),
+    "sg": ("sbuf", [128, 16], "float32"), "rn": ("sbuf", [128, 1], "float32"), "nb": ("sbuf", [128, 2], "float32"),
     "ex": ("sbuf", [128, 128], "float32"), "exT": ("sbuf", [128, 96], "float32"),
     "ns": ("sbuf", [128, 1], "float32"), "vs": ("sbuf", [128, 32], "float32"),
     "sgA": ("sbuf", [128, 512], "bfloat16"), "ge": ("sbuf", [128, 512], "bfloat16"),
@@ -48,8 +55,9 @@ SCRATCH = {
     "tokw": ("sbuf", [128, 48], "uint16"), "tokr": ("sbuf", [128, 48], "uint16"),
     "h": ("sbuf", [128, 3072], "bfloat16"), "rt": ("sbuf", [128, 3072], "bfloat16"),
     "tk": ("sbuf", [128, 512], "bfloat16"), "mr": ("sbuf", [128, 1088], "bfloat16"), "mT": ("sbuf", [128, 1088], "bfloat16"),
-    "pu": ("sbuf", [128, 34], "float32"), "pos": ("sbuf", [128, 34], "float32"), "oL": ("sbuf", [128, 68], "uint16"),
-    "G": ("sbuf", [128, 2304], "float32"), "P": ("sbuf", [128, 4 * PW], "float32"), "D": ("sbuf", [128, 768], "float32"),
+    "pu": ("sbuf", [128, 34], "float32"), "pos": ("sbuf", [128, 34], "float32"), "oL": ("sbuf", [128, LO[4]], "uint16"),
+    "fL": ("sbuf", [128, LO[4]], "float32"), "D3": ("sbuf", [128, 1024], "float32"),
+    "G": ("sbuf", [128, 2304], "float32"), "P": ("sbuf", [128, 4 * PW], "float32"), "D": ("sbuf", [128, 800], "float32"),
     "ys": ("sbuf", [128, 2048], "float32"),
 }
 for _b in range(8):
@@ -147,6 +155,8 @@ def rank_program(g, core, T, topo):
     SLOT = (0, 3, 2, 1)
     E = [1, 0, 2, 3] if 1 in O[2:] else [0, 1, 2, 3]
     B = [E.index(r) for r in O]
+    last = B[1]
+    late = last == 1
     eoff = topo.engines(core, T.cores[O[0]])
     eon = [e for e in topo.engines(core, T.cores[O[2]]) if e not in eoff] or eoff
     part = {O[0]: eoff, O[1]: eoff, O[2]: eon}
@@ -165,61 +175,99 @@ def rank_program(g, core, T, topo):
     ip = done("g", g.iota(T.ip[:], [[0, 32]], 0, 1))
     ic = done("g", g.iota(T.ic[:], [[4, 4], [0, 8]], 0, 0))
     on1 = ms(T.ones[:], 1.0)
+    ez = ms(T.et[:], 0.0)
+    need("g", [on1])
+    idn = done("g", g.affine_select(T.idn[:], T.ones[:], [[-1, 128]], A.is_equal, 0.0, 0, 1))
     t2 = ts(T.t2[:], T.ip[:], 3, A.bitwise_and, deps=[ip])
     ms(T.za[:, 16:48], BIG)
     l1 = tt(T.l1[:], T.ic[:], T.t2[:], A.add, [ic, t2])
     ms(T.zb[:, 16:48], -BIG)
     o1 = cp(T.o1[:], T.l1[:], [l1])
+    et = [act(T.et[:, 512 * b + b:512 * b + 512:4], T.idn[:], F.Copy, [ez, idn]) for b in range(4)]
     ms(T.cb[:, 0:16], 0.0)
     ms(T.dd[:, 511:512], float(CK))
     ms(T.X0[:], 0.0)
-    ms(T.nb[:], (NT - 2 * CK + 1) / 32 * BIG)
+    ms(T.nb[:, 0:1], (NT - 2 * CK + 1) / 32 * BIG)
+    ms(T.nb[:, 1:2], (NT - 2 * CK - 0.5) * BIG)
+    ms(T.D[:, 0:800:200], 0.0)
     pz = ms(T.P[:, 0:4 * PW:PW], 0.0)
     for e in range(NR):
         iota(quad(T.k2, e, 0, 8), [[64, 8]], 1, 2)
         kb = iota(quad(T.base, e, 0, 8), [[0, 8]], CK * E.index(e), 0)
-    et = []
-    for b in range(4):
-        need("g", [on1, kb])
-        et.append(done("g", g.affine_select(T.et[:, 512 * b:512 * b + 512], T.ones[:], [[1, 512]], A.is_equal, 0.0, -b, -4)))
+    eqd = quant(T.eq[:], T.ec[:], T.et[:], et)
 
     g1 = act(T.gl1[:], T.gs[:, 0:16].indirect(T.o1[:, 0:32]), F.Copy, [lg, o1])
     g1 = quant(T.g1q[:], T.g1c[:], T.gl1[:], [g1])
 
-    xq = [quant(T.xq[:, a:b], T.xc[:, a:b], T.xs[:, 4 * a:4 * b], [lx[i]]) for i, (a, b) in enumerate(XP)]
-    zV = mm(T.ps0[:], T.g1q[:], T.g1c[:], T.xq[:], T.xc[:], [g1] + xq)
-    zS = mm(T.ps1[:], T.g1q[:], T.g1c[:], T.xq[:], T.xc[:])
-    zt0 = tr(T.zT[:, 0:64], T.ps0[:, 0:64], [zV])
-    zt1 = tr(T.zT[:, 64:512], T.ps0[:, 64:512])
-    for c in range(NS):
-        aS = act(T.junk[:, 512 * c:512 * c + 512], T.ps1[:], F.Sign, [zS, zt0 if c < 2 else zt1],
-                 bias=T.zT[:, 32 * c:32 * c + 1], scale=-1.0, accum_out=T.accS[:, c:c + 1])
-    prev = None
+    def xquant(i):
+        a, b = XP[i]
+        return quant(T.xq[:, a:b], T.xc[:, a:b], T.xs[:, 4 * a:4 * b], [lx[i]])
+
+    def scores(bank, a, b, deps):
+        return mm(bank[:, 0:b - a], T.g1q[:], T.g1c[:], T.xq[:, a:b], T.xc[:, a:b], deps)
+
+    def sign(c, k, bank, a, n, deps):
+        return act(T.junk[:, 512 * c + a:512 * c + a + n], bank[:, 0:n], F.Sign, deps,
+                   bias=T.zT[:, 32 * c:32 * c + 1], scale=-1.0, accum_out=T.accS[:, k:k + 1])
+
+    def above(i, bank, a, n, deps):
+        c = NS + i
+        return ts(T.cmp[:, 512 * i + a:512 * i + a + n], bank[:, 0:n], T.zT[:, 32 * c:32 * c + 1], A.is_gt, BIG, A.mult, deps)
+    h0 = 32 * (8 - EV)
+    x0 = xquant(0)
+    zA, zA2 = scores(T.ps2, 0, 256, [g1, x0]), scores(T.ps4, 0, 256, [])
+    ta = tr(T.zT[:, 0:h0], T.ps2[:, 0:h0], [zA])
+    tb = tr(T.zT[:, 32 * NS:32 * (NS + EV)], T.ps2[:, h0:256])
+    for c in range(ES):
+        sign(c, c, T.ps4, 0, 256, [zA2, ta])
+    x1 = xquant(1)
+    above(0, T.ps2, 0, 256, [tb])
+    x2 = xquant(2)
+    zB, zB2 = scores(T.ps3, 256, 512, [x1, x2]), scores(T.ps5, 256, 512, [])
+    zS, zV = scores(T.ps1, 0, 512, []), scores(T.ps0, 0, 512, [])
+    for i in range(1, EV):
+        above(i, T.ps2, 0, 256, [])
+    tc = tr(T.zT[:, h0:32 * NS], T.ps3[:, 0:32 * NS - h0], [zB])
+    td = tr(T.zT[:, 32 * (NS + EV):512], T.ps3[:, 32 * NS - h0:256])
+    for c in range(ES):
+        aH = sign(c, NS + c, T.ps5, 256, 256, [zB2])
+    for c in range(ES, NS):
+        aS = sign(c, c, T.ps1, 0, 512, [zS, tc])
+    def wquant(i):
+        return quant(T.wq[:, 128 * i:128 * i + 128], T.wc[:, 128 * i:128 * i + 128], T.ws1[:, 512 * i:512 * i + 512], [lw])
+
+    prev, m1 = None, []
     for i in range(NV + 1):
         if i < NV:
-            c = NS + i
-            cur = ts(T.cmp[:, 512 * i:512 * i + 512], T.ps0[:], T.zT[:, 32 * c:32 * c + 1], A.is_gt, deps=[zt1])
+            cur = above(i, T.ps3, 256, 256, []) if i < EV else above(i, T.ps0, 0, 512, [zV, td])
+        else:
+            wquant(0)
         if i > 0:
             k = i - 1
-            wV = scan(T.scv[:, 256 * k:256 * k + 256], T.cmp[:, 512 * k:512 * k + 256], T.cmp[:, 512 * k + 256:512 * k + 512],
-                      0.5 - CK, A.add, A.add, [prev])
+            m1 = [scan(T.mk[:, NS + k + 255:NS + k - 1:-1], T.cmp[:, 512 * k:512 * k + 256],
+                       T.cmp[:, 512 * k + 256:512 * k + 512], (0.5 - CK) * BIG, A.add, A.add, [prev] + m1)]
+        if i == NV - 2:
+            aH = tt(T.accS[:, 0:ES], T.accS[:, 0:ES], T.accS[:, NS:NS + ES], A.add, [aH])
         prev = cur
-    m1 = ts(T.mk[:, NS:16], T.scv[:, 255:256 * NV:256], BIG, A.mult, deps=[wV])
-    m0 = ts(T.mk[:, 0:NS], T.accS[:], NT - 2 * CK - 0.5, A.subtract, -BIG, A.mult, [aS])
-    za = tt(T.za[:, 0:16], T.zT[:, 0:512:32], T.mk[:], A.max, [m0, m1])
-    zb = tt(T.zb[:, 0:16], T.zT[:, 0:512:32], T.mk[:], A.min)
-    rn = act(T.sg[:], T.mk[:], F.Sign, [m0, m1], accum_out=T.rn[:])
-    xn = act(T.ex[:, 48:80], T.zb[:, 16:48], F.Identity, [rn], scale=T.rn[:], bias=T.nb[:])
+    m0 = act(T.mk[:, 0:NS], T.accS[:, 0:NS], F.Identity, [aS, aH], scale=-BIG, bias=T.nb[:, 1:2])
+    za = tt(T.za[:, 0:16], T.zT[:, 0:512:32], T.mk[:, 0:16], A.max, [m0] + m1)
+    zb = tt(T.zb[:, 0:16], T.zT[:, 0:512:32], T.mk[:, 0:16], A.min)
+    rn = act(T.sg[:], T.mk[:, 0:16], F.Sign, [m0] + m1, accum_out=T.rn[:])
+    xn = act(T.ex[:, 48:80], T.zb[:, 16:48], F.Identity, [rn], scale=T.rn[:], bias=T.nb[:, 0:1])
     xa = scan(T.ex[:, 0:48], T.za[:], T.za[:], BIG, A.min, A.min, [za])
     xb = scan(T.ex[:, 127:79:-1], T.zb[:], T.zb[:], -BIG, A.max, A.max, [zb])
+    wquant(1)
     xt = tr(T.exT[:], T.ex[:, 16:112], [xa, xb, xn])
+    wquant(2)
     ns = red(T.ns[:], T.exT[:, 32:64], A.add, [xt])
+    wq = wquant(3)
     vs = scan(T.vs[:], T.exT[:, 0:32], T.exT[:, 64:96], T.ns[:], A.min, A.max, [ns])
     sA = act(T.sgA[:], T.ps1[:], F.Sign, [vs], bias=T.vs[:, 31:32], scale=-1.0)
-    ge = ts(T.ge[:], T.ps0[:], T.vs[:, 31:32], A.is_ge, deps=[vs])
-    gt = ts(T.gt[:], T.sgA[:], 0.0, A.is_lt, -1.0, A.mult, [sA])
+    gt = ts(T.gt[:], T.ps0[:], T.vs[:, 31:32], A.is_gt, -1.0, A.mult, [vs])
+    g0 = act(T.ge[:, 0:GS], T.sgA[:, 0:GS], F.Sign, [sA], bias=1.0, scale=-1.0)
+    g1 = ts(T.ge[:, GS:512], T.sgA[:, GS:512], 0.0, A.is_le, deps=[sA])
     dd = scan(T.dd[:, 510::-1], T.gt[:, 511:0:-1], T.gt[:, 511:0:-1], float(CK), A.add, A.max, [gt])
-    C = scan(T.cb[:, 16:528], T.ge[:], T.dd[:], 0.0, A.add, A.min, [dd, ge])
+    C = scan(T.cb[:, 16:528], T.ge[:], T.dd[:], 0.0, A.add, A.min, [dd, g0, g1])
     for c in range(CS):
         aS = act(T.jk2[:, WS * c:WS * c + WS], T.cb[:, 528 - WS:528], F.Sign, [C, kb],
                  bias=T.k2[:, CV + c:CV + c + 1], scale=-2.0, accum_out=T.acc2[:, c:c + 1])
@@ -233,6 +281,14 @@ def rank_program(g, core, T, topo):
             wV = scan(T.sc2[:, H * k:H * k + H], T.cm2[:, WV * k:WV * k + H], T.cm2[:, WV * k + H:WV * k + WV],
                       32.0 * k - 256.0, A.add, A.add, [prev])
         prev = cur
+    def marks():
+        for a in range(0, NT, 128):
+            tk = tt(T.tk[:, a:a + 128], T.cb[:, 16 + a:144 + a], T.cb[:, 15 + a:143 + a], A.subtract, [C])
+            yield tk
+        for a in range(0, NT, 128):
+            yield tt(T.mr[:, a:a + 128], T.cb[:, 16 + a:144 + a], T.tk[:, a:a + 128], A.mult, [tk])
+    mark = marks()
+    next(mark)
     x0 = []
     for o in range(NR):
         x0.append(act(T.X0[0:32, 6 * o + CV:6 * o + 6], quad(T.acc2, O[o], 0, CS), F.Identity, [aS, pz],
@@ -242,22 +298,30 @@ def rank_program(g, core, T, topo):
         x0.append(ts(out, src, 4.0, A.mult, 1024.0, A.add, [wV]) if o % 2 == 0 else
                   act(out, src, F.Identity, [wV], scale=4.0, bias=1024.0))
 
-    def wrap(n, W, Z, X, deps):
-        z = tr(Z[0:n, 16:48], X, deps)
+    def wrap(n, W, Z, z):
         d0 = cp(Z[0:n, 0:16], Z[0:n, 16:32], [z])
+        yield d0
         d1 = cp(Z[0:n, 48:64], Z[0:n, 32:48])
-        tr(W[0:n, 0:64:2], Z[0:n, 0:32], [d0])
-        return tr(W[0:n, 1:64:2], Z[0:n, 32:64], [d1])
-    w = wrap(32, T.W0, T.Z0, T.X0[0:32, 0:32], x0)
-    for a in range(4):
-        wr = cp(quad(T.tokw, a, 0, 48), T.W0[0:32, 0:48], [w])
+        yield d1
+        yield tr(W[0:n, 0:64:2], Z[0:n, 0:32], [d0])
+        yield tr(W[0:n, 1:64:2], Z[0:n, 32:64], [d1])
+    next(mark)
+    for a in range(2):
+        z = tr(quad(T.Z0, a, 16, 48), T.X0[0:32, 0:32], x0)
+    next(mark)
+    w = list(wrap(64, T.W0, T.Z0, z))[-1]
+    next(mark)
+    for a in range(2):
+        wr = cp(T.tokw[64 * a:64 * a + 64, :], T.W0[0:64, 0:48], [w])
+    mr = [next(mark)]
 
-    def gather(o):
+    def gather(o, on="vvss"):
         r = []
         for t in range(4):
             out = T.h[:, 768 * o + t:768 * o + 768:4]
             win = T.xs[:, 0:2048] if t == 0 else T["xs%d" % t][:, 16:2064 - t]
-            r.append(move("vvss"[t], out, win.indirect(T.tokw[:, 12 * o:12 * o + 12]), [wr] + lsh[t]))
+            r.append(move(on[t], out, win.indirect(T.tokw[:, 12 * o:12 * o + 12]), [wr] + lsh[t]))
+        mr[0] = next(mark, mr[0])
         return quant(T.sq[:, CK * o:CK * o + CK], T.sc[:, CK * o:CK * o + CK], T.h[:, 768 * o:768 * o + 768], r)
 
     def send(o, sb, sp, db, dp, sem, dep):
@@ -280,12 +344,11 @@ def rank_program(g, core, T, topo):
 
     for o in range(3):
         send(o, "sq", "sc", "rq", "rc", "rd", gather(o))
-    wq = quant(T.wq[:], T.wc[:], T.ws1[:], [lw])
-    qown = gather(3)
 
-    free = [[sA, ge], []]
+    free = [[sA, gt], [sA]]
+    lst = [None]
 
-    def expert(bset, cq, cc, o, qout, qsc, z, deps):
+    def expert(bset, cq, cc, o, qout, qsc, z, deps, k):
         rd, m = [], {}
         for i in (2, 0, 3, 1):
             m[i] = mm(T["ps%d" % (4 * bset + i)][:, 0:CK], T.wq[:, 128 * i:128 * i + 128], T.wc[:, 128 * i:128 * i + 128],
@@ -295,41 +358,61 @@ def rank_program(g, core, T, topo):
             src = T["ps%d" % (4 * bset + i)][:, 0:CK]
             if i < 2:
                 rd.append(ts(out, src, 0.0, A.max, 0.05, A.mult, [m[i]]))
+                fill(k if i == 0 else 0)
             else:
                 rd.append(act(out, src, F.Relu, [m[i]], scale=0.05))
         free[bset] = rd
         return quant(T[qout][:, CK * z:CK * z + CK], T[qsc][:, CK * z:CK * z + CK], T.rt[:, 768 * o:768 * o + 768], rd)
 
     tr4 = ts(T.tokr[:], T.tokw[:], 0.25, A.mult, deps=[wr])
-    tk = tt(T.tk[:], T.cb[:, 16:528], T.cb[:, 15:527], A.subtract, [C])
-    q3 = expert(1, "sq", "sc", 3, "bq", "bc", SLOT[3], [qown])
-    mr = tt(T.mr[:, 0:512], T.cb[:, 16:528], T.tk[:], A.mult, [tk])
-    for bset, o in ((0, 0), (1, 2), (0, 1)):
-        send(o, "oq", "oc", "bq", "bc", "rr", expert(bset, "rq", "rc", o, "oq", "oc", o, [arrived("rd", o)]))
+    qown = gather(3, OG)
+    tr(T.mT[:, 0:512], T.mr[:, 0:512], mr)
     for i in range(3):
         c0 = 12 * B.index(3 - i)
-        xl = act(T.mr[:, 512 + CK * i:512 + CK * (i + 1)], T.mr[:, 0:512].indirect(T.tokr[:, c0:c0 + 12]), F.Copy, [mr, tr4])
-    eqd = quant(T.eq[:], T.ec[:], T.et[:], et)
+        xl = act(T.mr[:, 512 + CK * i:512 + CK * (i + 1)], T.mr[:, 0:512].indirect(T.tokr[:, c0:c0 + 12]), F.Copy, mr + [tr4])
 
-    tr(T.mT[:, 0:512], T.mr[:, 0:512], [mr])
-    x = tr(T.mT[:, 512:1088], T.mr[:, 512:1088], [xl])
-    x = ts(T.pu[:], T.mT[:, 0:1088:32], 1024.0, A.mult, T.base[:, 0:1], A.min, [x])
-    x = tt(T.pos[:], T.pu[:], T.mT[:, 0:1088:32], A.add, [x])
-    for q, n in ((1, 28), (2, 22)):
-        x = tt(quad(T.pos, E[0], 0, n), quad(T.pos, E[0], 0, n), quad(T.pos, E[q], 0, n), A.max, [x])
-    tt(T.X0[0:32, 32:48], quad(T.pos, E[0], 0, 16), quad(T.pos, E[3], 0, 16), A.max, [x])
-    x = cp(T.X0[32:64, 32:50], quad(T.pos, E[0], 16, 34))
-    x = wrap(64, T.W1, T.Z1, T.X0[0:64, 32:64], [x])
+    n = 128 if late else 64
+
+    def lists():
+        x = tr(T.mT[:, 512:1088], T.mr[:, 512:1088], [xl])
+        yield x
+        x = ts(T.pu[:], T.mT[:, 0:1088:32], 1024.0, A.mult, T.base[:, 0:1], A.min, [x])
+        yield x
+        x = tt(T.pos[:], T.pu[:], T.mT[:, 0:1088:32], A.add, [x])
+        yield x
+        for q, m in ((1, 28), (2, 22)):
+            x = tt(quad(T.pos, E[0], 0, m), quad(T.pos, E[0], 0, m), quad(T.pos, E[q], 0, m), A.max, [x])
+            yield x
+        yield cp(T.X0[32:64, 32:50], quad(T.pos, E[0], 16, 34), [x])
+        if late:
+            yield cp(T.X0[64:96, 32:48], quad(T.pos, E[0], 0, 16))
+            yield cp(T.X0[96:128, 32:48], quad(T.mT, E[3], 0, 512, 32))
+        x = tt(T.X0[0:32, 32:48], quad(T.pos, E[0], 0, 16), quad(T.pos, E[3], 0, 16), A.max)
+        yield x
+        x = tr(T.Z1[0:n, 16:48], T.X0[0:n, 32:64], [x])
+        yield x
+        yield from wrap(n, T.W1, T.Z1, x)
+    todo = lists()
+
+    def fill(k):
+        for _ in range(k):
+            lst[0] = next(todo, lst[0])
+    fill(F0[0])
+    q3 = expert(1, "sq", "sc", 3, "bq", "bc", SLOT[3], [qown], F0[1])
+    fill(FILL[0])
+    for k, (bset, o) in enumerate(((0, 0), (1, 2), (0, 1))):
+        send(o, "oq", "oc", "bq", "bc", "rr", expert(bset, "rq", "rc", o, "oq", "oc", o, [arrived("rd", o)], FI))
+        fill(FILL[k + 1])
+    y = [move("vs"[a], quad(T.fL, a, LO[i], LO[i + 1]), quad(T.W1, i, 0, LO[i + 1] - LO[i]), lst)
+         for i in range(n // 32) for a in range(2)]
     for a in range(2):
-        cp(quad(T.oL, a, 0, 32), T.W1[0:32, 0:32], [x])
-        y = cp(quad(T.oL, a, 32, 68), T.W1[32:64, 0:36])
-    oL = cp(T.oL[64:128, :], T.oL[0:64, :], [y])
+        oL = cp(T.oL[64 * a:64 * a + 64, 0:LO[n // 32]], T.fL[0:64, 0:LO[n // 32]], y)
 
     dm, got, gs, sb = {}, {}, {}, {}
 
-    def decode(bset, z, blocks, deps):
+    def decode(bset, z, blocks, deps, rows=range(4)):
         n = len(blocks) * CK
-        for b in range(4):
+        for b in rows:
             m = mm(T["ps%d" % (4 * bset + b)][:, 0:n], T.eq[:, 128 * b:128 * b + 128], T.ec[:, 128 * b:128 * b + 128],
                    T.bq[:, CK * z:CK * z + n], T.bc[:, CK * z:CK * z + n], deps[b] + [eqd])
             for i, q in enumerate(blocks):
@@ -341,8 +424,8 @@ def rank_program(g, core, T, topo):
     def earlier(q, b):
         return T.P[:, PW * b:PW * b + 1 + CK * q].indirect(T.oL[:, 68 - 12 * q:80 - 12 * q])
 
-    def first():
-        for b in range(4):
+    def first(rows=range(4)):
+        for b in rows:
             got[b] = move("svsv"[b], slots(0, b), dm[(0, b)][1], [dm[(0, b)][0]])
 
     def pick(q, b, on):
@@ -353,44 +436,79 @@ def rank_program(g, core, T, topo):
         m, src = dm[(q, b)]
         got[b] = tt(slots(q, b), src, gs[b][1], A.add, [m, gs[b][0], got[b]])
 
+    def parked(q, b, a=1):
+        c0 = 200 * (2 * (q - 2) + b - 2)
+        return T.D[:, c0 + a:c0 + 1 + CK]
+
     def park(q):
-        sb[q] = act(T.D[:, CK * q:CK * q + CK], dm[(q, FB)][1], F.Copy, [dm[(q, FB)][0]])
+        for b in FB:
+            sb[(q, b)] = move("vs"[b - 2], parked(q, b), dm[(q, b)][1], [dm[(q, b)][0]])
+        return [sb[(q, b)] for b in FB]
 
     def after(extra=()):
         return [[got[b]] + list(extra) for b in range(4)]
 
-    last = B[1]
-    if B[3] == 0:
+    def fused(q, b):
+        got[b] = tt(slots(q, b), earlier(q, b), parked(q, b), A.add, [got[b], sb[(q, b)]])
+
+    def tokens(b, n, i, a, z):
+        return T.P[:, PW * b:PW * b + 1 + n * CK].indirect(T.oL[:, LO[i] + a // 16:LO[i] + z // 16])
+
+    rest = (1, 0)
+    if not late:
         decode(0, 1, [0], [[q3] + free[0]] * 4)
         first()
         decode(0, 0, [1], after([arrived("rr", 0)]))
         decode(1, 2, [B[2]], [[arrived("rr", 2)] + free[1]] * 4)
-        lastset = 0
+        for q in range(1, last + 1):
+            if q == last:
+                decode(0, 3, [q], after([arrived("rr", 1)]), rest + FB)
+            for b in rest + FB:
+                pick(q, b, "sssv"[b])
+            if q == last and q < 3:
+                park(3)
+            for b in rest + FB:
+                add(q, b)
+        if last < 3:
+            for b in rest:
+                pick(3, b, "s")
+            for b, c in zip(FB, rest):
+                fused(3, b)
+                add(3, c)
     else:
-        decode(0, 2, [0], [[arrived("rr", 2)] + free[0]] * 4)
-        first()
-        decode(0, 0, [B[0], B[3]], after([arrived("rr", 0), q3]))
-        lastset = 1
-    for q in range(1, last + 1):
-        for b in range(4):
-            pick(q, b, "vsss"[b])
-        if q == last:
-            for p in range(last + 1, NR):
-                park(p)
-            decode(lastset, 3, [q], after([arrived("rr", 1)] + free[lastset]))
-        for b in range(4):
-            add(q, b)
-    for q in range(last + 1, NR):
-        rest = [b for b in range(4) if b != FB]
+        used, d3 = list(free[1]), {}
+        for q, z, dep in ((B[3], 1, q3), (B[0], 0, arrived("rr", 0))):
+            decode(1, z, [q], [[dep] + used] * 4, FB[::-1])
+            used = park(q)
+        decode(0, 2, [0], [[arrived("rr", 2)] + free[0]] * 4, rest + FB)
+        for b in FB:
+            d3[b] = move("vs"[b - 2], T.D3[:, 512 * (b - 2):512 * (b - 1)], parked(3, b, 0).indirect(T.oL[:, LO[3]:LO[4]]),
+                         [sb[(3, b)], oL])
+        first(rest + FB)
+        decode(0, 1, [B[3]], after(), rest)
+        for b in rest + FB:
+            pick(1, b, "svsv"[b])
+        decode(1, 3, [1], [[arrived("rr", 1)] + used] * 4, rest + FB)
+        for b in rest + FB:
+            add(1, b)
+        decode(1, 0, [B[0]], after(), rest)
         for b in rest:
-            pick(q, b, "s")
-        got[FB] = tt(slots(q, FB), earlier(q, FB), T.D[:, CK * q:CK * q + CK], A.add, [got[FB], sb[q]])
+            pick(2, b, "s")
         for b in rest:
-            add(q, b)
+            add(2, b)
+        for b in rest:
+            pick(3, b, "s")
+        for b in FB:
+            fused(2, b)
+        for b in rest:
+            add(3, b)
     for a, z in YP:
         r = []
-        for b, on in ((FB, "s"), (0, "s"), (1, "v"), (2, "v")):
-            src = T.P[:, PW * b:PW * b + 1 + NR * CK].indirect(T.oL[:, a // 16:z // 16])
-            r.append(move(on, T.ys[:, 4 * a + b:4 * z:4], src, [got[b], oL]))
+        for b in rest + FB:
+            out = T.ys[:, 4 * a + b:4 * z:4]
+            if late and b in FB:
+                r.append(tt(out, tokens(b, 3, 2, a, z), T.D3[:, 512 * (b - 2) + a:512 * (b - 2) + z], A.add, [got[b], d3[b]]))
+            else:
+                r.append(move("ssvv"[b], out, tokens(b, 4, 0, a, z), [got[b], oL]))
         st = dma("y", "sty", T.y[:, 4 * a:4 * z], T.ys[:, 4 * a:4 * z], r)
     need("y", [(k, n) for k, n in tot.items()] + [("c" + k, n) for k, n in cnt.items()])

@@ -15,9 +15,12 @@ XP = ((0, 256), (256, 384), (384, 512))
 YP = ((0, 64), (64, 160), (160, 320), (320, 512))
 GS = 352
 FI = 1
+DO = (0, 1, 2)
+EO = (0, 2, 1)
 F0 = (0, 1)
 OG = "vsss"
-FILL = (5, 0, 2, 99)
+P1, P2 = "svsv", "svss"
+FILL = (3, 1, 1, 0)
 LO = (0, 32, 68, 100, 132)
 BIG = 2.0 ** 86
 FB = (3, 2)
@@ -150,13 +153,13 @@ def rank_program(g, core, T, topo):
         near = [k for k in range(NR) if topo.chip(T.cores[k]) == topo.chip(c)]
         off = [k for k in range(NR) if k not in near]
         i = near.index(r)
-        return [off[i], off[1 - i]] + [k for k in near if k != r] + [r]
+        return [off[1 - i], off[i]] + [k for k in near if k != r] + [r]
     O = order(me)
-    SLOT = (0, 3, 2, 1)
-    E = [1, 0, 2, 3] if 1 in O[2:] else [0, 1, 2, 3]
+    come = [O[3], O[0], O[2], O[1]]
+    E = sorted((0, 1), key=come.index) + [2, 3]
     B = [E.index(r) for r in O]
     last = B[1]
-    late = last == 1
+    late = last < 3
     eoff = topo.engines(core, T.cores[O[0]])
     eon = [e for e in topo.engines(core, T.cores[O[2]]) if e not in eoff] or eoff
     part = {O[0]: eoff, O[1]: eoff, O[2]: eon}
@@ -175,16 +178,16 @@ def rank_program(g, core, T, topo):
     ip = done("g", g.iota(T.ip[:], [[0, 32]], 0, 1))
     ic = done("g", g.iota(T.ic[:], [[4, 4], [0, 8]], 0, 0))
     on1 = ms(T.ones[:], 1.0)
-    ez = ms(T.et[:], 0.0)
+    ez = ms(T.et[:, 0:1024], 0.0)
+    ez = act(T.et[:, 1024:2048], T.et[:, 0:1024], F.Copy, [ez])
     need("g", [on1])
     idn = done("g", g.affine_select(T.idn[:], T.ones[:], [[-1, 128]], A.is_equal, 0.0, 0, 1))
-    t2 = ts(T.t2[:], T.ip[:], 3, A.bitwise_and, deps=[ip])
     ms(T.za[:, 16:48], BIG)
-    l1 = tt(T.l1[:], T.ic[:], T.t2[:], A.add, [ic, t2])
+    t2 = ts(T.t2[:], T.ip[:], 3, A.bitwise_and, deps=[ip])
     ms(T.zb[:, 16:48], -BIG)
-    o1 = cp(T.o1[:], T.l1[:], [l1])
-    et = [act(T.et[:, 512 * b + b:512 * b + 512:4], T.idn[:], F.Copy, [ez, idn]) for b in range(4)]
+    l1 = tt(T.l1[:], T.ic[:], T.t2[:], A.add, [ic, t2])
     ms(T.cb[:, 0:16], 0.0)
+    o1 = cp(T.o1[:], T.l1[:], [l1])
     ms(T.dd[:, 511:512], float(CK))
     ms(T.X0[:], 0.0)
     ms(T.nb[:, 0:1], (NT - 2 * CK + 1) / 32 * BIG)
@@ -194,10 +197,10 @@ def rank_program(g, core, T, topo):
     for e in range(NR):
         iota(quad(T.k2, e, 0, 8), [[64, 8]], 1, 2)
         kb = iota(quad(T.base, e, 0, 8), [[0, 8]], CK * E.index(e), 0)
-    eqd = quant(T.eq[:], T.ec[:], T.et[:], et)
-
-    g1 = act(T.gl1[:], T.gs[:, 0:16].indirect(T.o1[:, 0:32]), F.Copy, [lg, o1])
-    g1 = quant(T.g1q[:], T.g1c[:], T.gl1[:], [g1])
+    g1 = [move("vs"[a], T.gl1[:, 256 * a:256 * a + 256], T.gs[:, 0:16].indirect(T.o1[:, 16 * a:16 * a + 16]), [lg, o1])
+          for a in range(2)]
+    g1 = quant(T.g1q[:], T.g1c[:], T.gl1[:], g1)
+    et = [act(T.et[:, 512 * b + b:512 * b + 512:4], T.idn[:], F.Copy, [ez, idn]) for b in range(4)]
 
     def xquant(i):
         a, b = XP[i]
@@ -216,6 +219,7 @@ def rank_program(g, core, T, topo):
     h0 = 32 * (8 - EV)
     x0 = xquant(0)
     zA, zA2 = scores(T.ps2, 0, 256, [g1, x0]), scores(T.ps4, 0, 256, [])
+    eqd = quant(T.eq[:, 0:256], T.ec[:, 0:256], T.et[:, 0:1024], et[0:2])
     ta = tr(T.zT[:, 0:h0], T.ps2[:, 0:h0], [zA])
     tb = tr(T.zT[:, 32 * NS:32 * (NS + EV)], T.ps2[:, h0:256])
     for c in range(ES):
@@ -262,11 +266,13 @@ def rank_program(g, core, T, topo):
     ns = red(T.ns[:], T.exT[:, 32:64], A.add, [xt])
     wq = wquant(3)
     vs = scan(T.vs[:], T.exT[:, 0:32], T.exT[:, 64:96], T.ns[:], A.min, A.max, [ns])
+    quant(T.eq[:, 256:384], T.ec[:, 256:384], T.et[:, 1024:1536], et)
     sA = act(T.sgA[:], T.ps1[:], F.Sign, [vs], bias=T.vs[:, 31:32], scale=-1.0)
     gt = ts(T.gt[:], T.ps0[:], T.vs[:, 31:32], A.is_gt, -1.0, A.mult, [vs])
     g0 = act(T.ge[:, 0:GS], T.sgA[:, 0:GS], F.Sign, [sA], bias=1.0, scale=-1.0)
     g1 = ts(T.ge[:, GS:512], T.sgA[:, GS:512], 0.0, A.is_le, deps=[sA])
     dd = scan(T.dd[:, 510::-1], T.gt[:, 511:0:-1], T.gt[:, 511:0:-1], float(CK), A.add, A.max, [gt])
+    eqd = quant(T.eq[:, 384:512], T.ec[:, 384:512], T.et[:, 1536:2048])
     C = scan(T.cb[:, 16:528], T.ge[:], T.dd[:], 0.0, A.add, A.min, [dd, g0, g1])
     for c in range(CS):
         aS = act(T.jk2[:, WS * c:WS * c + WS], T.cb[:, 528 - WS:528], F.Sign, [C, kb],
@@ -281,6 +287,7 @@ def rank_program(g, core, T, topo):
             wV = scan(T.sc2[:, H * k:H * k + H], T.cm2[:, WV * k:WV * k + H], T.cm2[:, WV * k + H:WV * k + WV],
                       32.0 * k - 256.0, A.add, A.add, [prev])
         prev = cur
+
     def marks():
         for a in range(0, NT, 128):
             tk = tt(T.tk[:, a:a + 128], T.cb[:, 16 + a:144 + a], T.cb[:, 15 + a:143 + a], A.subtract, [C])
@@ -327,8 +334,6 @@ def rank_program(g, core, T, topo):
     def send(o, sb, sp, db, dp, sem, dep):
         r = O[o]
         p = order(r).index(me)
-        if sem == "rr":
-            p = SLOT[p]
         rid, pid, _ = topo.addr(T.cores[r])
         need("g", [dep])
         for a, b, code in ((sb, db, True), (sp, dp, False)):
@@ -342,7 +347,7 @@ def rank_program(g, core, T, topo):
     def arrived(sem, o):
         return (sem + str(O[o]), 2 * len(part[O[o]]))
 
-    for o in range(3):
+    for o in DO:
         send(o, "sq", "sc", "rq", "rc", "rd", gather(o))
 
     free = [[sA, gt], [sA]]
@@ -398,25 +403,26 @@ def rank_program(g, core, T, topo):
         for _ in range(k):
             lst[0] = next(todo, lst[0])
     fill(F0[0])
-    q3 = expert(1, "sq", "sc", 3, "bq", "bc", SLOT[3], [qown], F0[1])
+    q3 = expert(1, "sq", "sc", 3, "bq", "bc", 3, [qown], F0[1])
     fill(FILL[0])
-    for k, (bset, o) in enumerate(((0, 0), (1, 2), (0, 1))):
+    for k, (bset, o) in enumerate(zip((0, 1, 0), EO)):
         send(o, "oq", "oc", "bq", "bc", "rr", expert(bset, "rq", "rc", o, "oq", "oc", o, [arrived("rd", o)], FI))
         fill(FILL[k + 1])
-    y = [move("vs"[a], quad(T.fL, a, LO[i], LO[i + 1]), quad(T.W1, i, 0, LO[i + 1] - LO[i]), lst)
-         for i in range(n // 32) for a in range(2)]
-    for a in range(2):
-        oL = cp(T.oL[64 * a:64 * a + 64, 0:LO[n // 32]], T.fL[0:64, 0:LO[n // 32]], y)
 
     dm, got, gs, sb = {}, {}, {}, {}
+    read = {k: free[k // 4] for k in range(8)}
 
-    def decode(bset, z, blocks, deps, rows=range(4)):
-        n = len(blocks) * CK
-        for b in rows:
-            m = mm(T["ps%d" % (4 * bset + b)][:, 0:n], T.eq[:, 128 * b:128 * b + 128], T.ec[:, 128 * b:128 * b + 128],
-                   T.bq[:, CK * z:CK * z + n], T.bc[:, CK * z:CK * z + n], deps[b] + [eqd])
-            for i, q in enumerate(blocks):
-                dm[(q, b)] = (m, T["ps%d" % (4 * bset + b)][:, CK * i:CK * i + CK])
+    def decode(o, rows, banks):
+        for b, k in zip(rows, banks):
+            m = mm(T["ps%d" % k][:, 0:CK], T.eq[:, 128 * b:128 * b + 128], T.ec[:, 128 * b:128 * b + 128],
+                   T.bq[:, CK * o:CK * o + CK], T.bc[:, CK * o:CK * o + CK],
+                   [q3 if o == 3 else arrived("rr", o), eqd] + read[k])
+            dm[(B[o], b)] = (m, k)
+
+    def take(q, b, call):
+        m, k = dm[(q, b)]
+        read[k] = [call(T["ps%d" % k][:, 0:CK], m)]
+        return read[k][0]
 
     def slots(q, b):
         return T.P[:, PW * b + 1 + CK * q:PW * b + 1 + CK * (q + 1)]
@@ -424,29 +430,31 @@ def rank_program(g, core, T, topo):
     def earlier(q, b):
         return T.P[:, PW * b:PW * b + 1 + CK * q].indirect(T.oL[:, 68 - 12 * q:80 - 12 * q])
 
-    def first(rows=range(4)):
+    def first(rows):
         for b in rows:
-            got[b] = move("svsv"[b], slots(0, b), dm[(0, b)][1], [dm[(0, b)][0]])
+            got[b] = take(0, b, lambda src, m: move("svsv"[b], slots(0, b), src, [m]))
 
-    def pick(q, b, on):
-        out = T.G[:, 768 * (q - 1) + CK * b:768 * (q - 1) + CK * b + CK]
-        gs[b] = (move(on, out, earlier(q, b), [got[b], oL]), out)
+    def pick(q, rows, on):
+        for b in rows:
+            out = T.G[:, 768 * (q - 1) + CK * b:768 * (q - 1) + CK * b + CK]
+            gs[b] = (move(on[b], out, earlier(q, b), [got[b], oL]), out)
 
-    def add(q, b):
-        m, src = dm[(q, b)]
-        got[b] = tt(slots(q, b), src, gs[b][1], A.add, [m, gs[b][0], got[b]])
+    def add(q, rows):
+        for b in rows:
+            got[b] = take(q, b, lambda src, m: tt(slots(q, b), src, gs[b][1], A.add, [m, gs[b][0], got[b]]))
 
     def parked(q, b, a=1):
         c0 = 200 * (2 * (q - 2) + b - 2)
         return T.D[:, c0 + a:c0 + 1 + CK]
 
-    def park(q):
-        for b in FB:
-            sb[(q, b)] = move("vs"[b - 2], parked(q, b), dm[(q, b)][1], [dm[(q, b)][0]])
-        return [sb[(q, b)] for b in FB]
+    def park(q, rows=FB[::-1]):
+        for b in rows:
+            sb[(q, b)] = take(q, b, lambda src, m: move("vs"[b - 2], parked(q, b), src, [m]))
 
-    def after(extra=()):
-        return [[got[b]] + list(extra) for b in range(4)]
+    def spread(q):
+        if q == 3:
+            bytoken(2, 0, 512)
+            bytoken(3, 0, 512 if B[3] == 3 else 256)
 
     def fused(q, b):
         got[b] = tt(slots(q, b), earlier(q, b), parked(q, b), A.add, [got[b], sb[(q, b)]])
@@ -454,60 +462,68 @@ def rank_program(g, core, T, topo):
     def tokens(b, n, i, a, z):
         return T.P[:, PW * b:PW * b + 1 + n * CK].indirect(T.oL[:, LO[i] + a // 16:LO[i] + z // 16])
 
-    rest = (1, 0)
-    if not late:
-        decode(0, 1, [0], [[q3] + free[0]] * 4)
-        first()
-        decode(0, 0, [1], after([arrived("rr", 0)]))
-        decode(1, 2, [B[2]], [[arrived("rr", 2)] + free[1]] * 4)
-        for q in range(1, last + 1):
-            if q == last:
-                decode(0, 3, [q], after([arrived("rr", 1)]), rest + FB)
-            for b in rest + FB:
-                pick(q, b, "sssv"[b])
-            if q == last and q < 3:
-                park(3)
-            for b in rest + FB:
-                add(q, b)
-        if last < 3:
-            for b in rest:
-                pick(3, b, "s")
-            for b, c in zip(FB, rest):
-                fused(3, b)
-                add(3, c)
+    def bytoken(b, a, z):
+        src = parked(3, b, 0).indirect(T.oL[:, LO[3] + a // 16:LO[3] + z // 16])
+        d3.append((b, a, move("vs"[b - 2], T.D3[:, 512 * (b - 2) + a:512 * (b - 2) + z], src, [sb[(3, b)], oL])))
+
+    rest, d3 = (1, 0), []
+    rows = rest + FB
+    if last == 1:
+        decode(3, rows, (4, 5, 6, 7))
+        own = [lambda: first(rest), lambda: first(FB)]
     else:
-        used, d3 = list(free[1]), {}
-        for q, z, dep in ((B[3], 1, q3), (B[0], 0, arrived("rr", 0))):
-            decode(1, z, [q], [[dep] + used] * 4, FB[::-1])
-            used = park(q)
-        decode(0, 2, [0], [[arrived("rr", 2)] + free[0]] * 4, rest + FB)
-        for b in FB:
-            d3[b] = move("vs"[b - 2], T.D3[:, 512 * (b - 2):512 * (b - 1)], parked(3, b, 0).indirect(T.oL[:, LO[3]:LO[4]]),
-                         [sb[(3, b)], oL])
-        first(rest + FB)
-        decode(0, 1, [B[3]], after(), rest)
-        for b in rest + FB:
-            pick(1, b, "svsv"[b])
-        decode(1, 3, [1], [[arrived("rr", 1)] + used] * 4, rest + FB)
-        for b in rest + FB:
-            add(1, b)
-        decode(1, 0, [B[0]], after(), rest)
-        for b in rest:
-            pick(2, b, "s")
-        for b in rest:
-            add(2, b)
-        for b in rest:
-            pick(3, b, "s")
+        decode(3, FB[::-1], (6, 7))
+        own = [lambda: park(B[3]), lambda: None]
+    fill(1)
+    own[0]()
+    fill(99)
+    own[1]()
+    y = [move("vs"[a], quad(T.fL, a, LO[i], LO[i + 1]), quad(T.W1, i, 0, LO[i + 1] - LO[i]), lst)
+         for i in range(n // 32) for a in range(2)]
+    for a in range(2):
+        oL = cp(T.oL[64 * a:64 * a + 64, 0:LO[n // 32]], T.fL[0:64, 0:LO[n // 32]], y)
+    if last == 1:
+        pick(1, rows, "svsv")
+        for o, k in ((0, 0), (2, 4)):
+            decode(o, FB[::-1] + rest, range(k, k + 4))
+            park(B[o])
+            spread(B[o])
+        decode(1, rows, (0, 1, 4, 5))
+        add(1, rows)
+        pick(2, rest, "ss")
+        add(2, rest)
+        pick(3, rest, "ss")
+        bytoken(3, 256, 512)
         for b in FB:
             fused(2, b)
-        for b in rest:
-            add(3, b)
+        add(3, rest)
+    else:
+        spread(B[3])
+        decode(0, rows, (0, 1, 2, 3))
+        first(rows)
+        decode(2, rows, (4, 5, 6, 7))
+        pick(1, rows, P1)
+        add(1, rows)
+        if not late:
+            decode(3, rest, (0, 1))
+            pick(2, rest, "ss")
+            for b, c in zip(FB, rest):
+                fused(2, b)
+                add(2, [c])
+        pick(last, rows if late else FB + rest, P2)
+        decode(1, rows, (0, 1, 2, 3) if late else (4, 5, 6, 7))
+        add(last, rows if late else FB + rest)
+        if late:
+            decode(3, rest, (4, 5))
+            pick(3, rest, "ss")
+            add(3, rest)
     for a, z in YP:
         r = []
         for b in rest + FB:
             out = T.ys[:, 4 * a + b:4 * z:4]
             if late and b in FB:
-                r.append(tt(out, tokens(b, 3, 2, a, z), T.D3[:, 512 * (b - 2) + a:512 * (b - 2) + z], A.add, [got[b], d3[b]]))
+                r.append(tt(out, tokens(b, 3, 2, a, z), T.D3[:, 512 * (b - 2) + a:512 * (b - 2) + z], A.add,
+                            [got[b]] + [d for c, s, d in d3 if c == b and s < z]))
             else:
                 r.append(move("ssvv"[b], out, tokens(b, 4, 0, a, z), [got[b], oL]))
         st = dma("y", "sty", T.y[:, 4 * a:4 * z], T.ys[:, 4 * a:4 * z], r)

from concourse.mybir import dt, AluOpType, AxisListType, ActivationFunctionType

A = AluOpType
F = ActivationFunctionType
NR, CK, NT = 4, 192, 512
NS = 9
NV = 16 - NS
ES, EV = 4, 3
CV = 4
CS = 6 - CV
WV = NT - CK + 32
WS = NT - 32 * CV
PW = 8 + NR * CK
XP = ((0, 256), (256, 384), (384, 512))
YP = ((0, 64), (64, 160), (160, 320), (320, 512))
GS = 352
FI = 1
DO = (0, 1, 2)
EO = (0, 2, 1)
F0 = (0, 1)
OG = "vsss"
P1, P2 = "svsv", "svss"
FILL = (3, 1, 1, 0)
LO = (0, 32, 68, 100, 132)
BIG = 2.0 ** 86
FB = (3, 2)

SCRATCH = {
    "xs": ("sbuf", [128, 2048], "bfloat16"), "xs1": ("sbuf", [128, 2064], "bfloat16"),
    "xs2": ("sbuf", [128, 2064], "bfloat16"), "xs3": ("sbuf", [128, 2064], "bfloat16"),
    "ws1": ("sbuf", [128, 2048], "bfloat16"),
    "gs": ("sbuf", [128, 16], "bfloat16"), "gl1": ("sbuf", [128, 512], "bfloat16"),
    "xq": ("sbuf", [128, 512], "float8_e4m3fn_x4"), "xc": ("sbuf", [128, 512], "uint8"),
    "wq": ("sbuf", [128, 512], "float8_e4m3fn_x4"), "wc": ("sbuf", [128, 512], "uint8"),
    "eq": ("sbuf", [128, 512], "float8_e4m3fn_x4"), "ec": ("sbuf", [128, 512], "uint8"),
    "g1q": ("sbuf", [128, 128], "float8_e4m3fn_x4"), "g1c": ("sbuf", [128, 128], "uint8"),
    "sq": ("sbuf", [128, 768], "float8_e4m3fn_x4"), "sc": ("sbuf", [128, 768], "uint8"),
    "rq": ("sbuf", [128, 576], "float8_e4m3fn_x4"), "rc": ("sbuf", [128, 576], "uint8"),
    "oq": ("sbuf", [128, 768], "float8_e4m3fn_x4"), "oc": ("sbuf", [128, 768], "uint8"),
    "bq": ("sbuf", [128, 768], "float8_e4m3fn_x4"), "bc": ("sbuf", [128, 768], "uint8"),
    "ones": ("sbuf", [128, 128], "bfloat16"), "idn": ("sbuf", [128, 128], "bfloat16"), "et": ("sbuf", [128, 2048], "bfloat16"),
    "ip": ("sbuf", [128, 32], "int32"), "ic": ("sbuf", [128, 32], "int32"),
    "t2": ("sbuf", [128, 32], "int32"), "l1": ("sbuf", [128, 32], "int32"), "o1": ("sbuf", [128, 32], "uint16"),
    "k2": ("sbuf", [128, 8], "float32"), "base": ("sbuf", [128, 8], "float32"),
    "zT": ("sbuf", [128, 512], "float32"), "junk": ("sbuf", [128, 512 * NS], "bfloat16"),
    "accS": ("sbuf", [128, NS + ES], "float32"),
    "cmp": ("sbuf", [128, 512 * NV], "bfloat16"),
    "mk": ("sbuf", [128, 272], "bfloat16"), "za": ("sbuf", [128, 48], "float32"), "zb": ("sbuf", [128, 48], "float32"),
    "sg": ("sbuf", [128, 16], "float32"), "rn": ("sbuf", [128, 1], "float32"), "nb": ("sbuf", [128, 2], "float32"),
    "ex": ("sbuf", [128, 128], "float32"), "exT": ("sbuf", [128, 96], "float32"),
    "ns": ("sbuf", [128, 1], "float32"), "vs": ("sbuf", [128, 32], "float32"),
    "sgA": ("sbuf", [128, 512], "bfloat16"), "ge": ("sbuf", [128, 512], "bfloat16"),
    "gt": ("sbuf", [128, 512], "bfloat16"), "dd": ("sbuf", [128, 512], "bfloat16"), "cb": ("sbuf", [128, 528], "bfloat16"),
    "jk2": ("sbuf", [128, WS * CS], "bfloat16"), "acc2": ("sbuf", [128, CS], "float32"),
    "cm2": ("sbuf", [128, WV * CV], "bfloat16"), "sc2": ("sbuf", [128, WV // 2 * CV], "bfloat16"),
    "X0": ("sbuf", [128, 64], "float32"), "Z0": ("sbuf", [128, 64], "float32"), "W0": ("sbuf", [128, 64], "float32"),
    "Z1": ("sbuf", [128, 64], "float32"), "W1": ("sbuf", [128, 64], "float32"),
    "tokw": ("sbuf", [128, 48], "uint16"), "tokr": ("sbuf", [128, 48], "uint16"),
    "h": ("sbuf", [128, 3072], "bfloat16"), "rt": ("sbuf", [128, 3072], "bfloat16"),
    "tk": ("sbuf", [128, 512], "bfloat16"), "mr": ("sbuf", [128, 1088], "bfloat16"), "mT": ("sbuf", [128, 1088], "bfloat16"),
    "pu": ("sbuf", [128, 34], "float32"), "pos": ("sbuf", [128, 34], "float32"), "oL": ("sbuf", [128, LO[4]], "uint16"),
    "fL": ("sbuf", [128, LO[4]], "float32"), "D3": ("sbuf", [128, 1024], "float32"),
    "G": ("sbuf", [128, 2304], "float32"), "P": ("sbuf", [128, 4 * PW], "float32"), "D": ("sbuf", [128, 800], "float32"),
    "ys": ("sbuf", [128, 2048], "float32"),
}
for _b in range(8):
    SCRATCH["ps%d" % _b] = ("psum", [128, 512], "float32")
SEMAPHORES = ["cv", "cs", "ct", "cg", "lx0", "lx1", "lx2", "lh1", "lh2", "lh3", "lg", "lw",
              "sty", "sent", "rd0", "rd1", "rd2", "rd3", "rr0", "rr1", "rr2", "rr3"]


def rank_program(g, core, T, topo):
    me = T.rank_of(core)
    if me is None:
        return
    S = T.sem
    Q = {"v": g.vector, "s": g.scalar, "t": g.tensor, "g": g, "y": g.sync}
    cnt, waited, tot = {}, {}, {}

    def need(q, deps):
        best = {}
        for sem, val in deps:
            best[sem] = max(val, best.get(sem, 0))
        for sem, val in best.items():
            if waited.get((q, sem), 0) < val:
                Q[q].wait_ge(S[sem], val)
                waited[(q, sem)] = val

    def done(q, ins):
        cnt[q] = cnt.get(q, 0) + 1
        ins.then_inc(S["c" + q], 1)
        return ("c" + q, cnt[q])

    def ts(out, in0, s1, op0, s2=None, op1=None, deps=()):
        need("v", deps)
        if op1 is None:
            return done("v", g.vector.tensor_scalar(out, in0, s1, None, op0))
        return done("v", g.vector.tensor_scalar(out, in0, s1, s2, op0, op1))

    def tt(out, a, b, op, deps=()):
        need("v", deps)
        return done("v", g.vector.tensor_tensor(out, a, b, op))

    def cp(out, a, deps=()):
        need("v", deps)
        return done("v", g.vector.tensor_copy(out, a))

    def ms(out, c):
        return done("v", g.vector.memset(out, c))

    def red(out, a, op, deps=()):
        need("v", deps)
        return done("v", g.vector.tensor_reduce(out, a, AxisListType.X, op))

    def scan(out, a, b, init, op0, op1, deps=()):
        need("v", deps)
        return done("v", g.vector.tensor_tensor_scan(out, a, b, init, op0, op1))

    def tr(out, a, deps=()):
        need("v", deps)
        return done("v", g.vector.transpose(out, a))

    def quant(out, sc, a, deps=()):
        need("v", deps)
        return done("v", g.vector.quantize_mx(out, sc, a))

    def act(out, a, func, deps=(), **kw):
        need("s", deps)
        return done("s", g.scalar.activation(out, a, func, **kw))

    def mm(out, l, ls, r, rs, deps=()):
        need("t", deps)
        return done("t", g.tensor.matmul_mx(out, l, ls, r, rs, True, True))

    def dma(q, sem, out, in_, deps=()):
        need(q, deps)
        Q[q].dma_start(out, in_).then_inc(S[sem], 16)
        tot[sem] = tot.get(sem, 0) + 16
        return (sem, tot[sem])

    def iota(out, pattern, base, cm):
        need("g", [("cg", cnt["g"])])
        return done("g", g.iota(out, pattern, base, cm, allow_small_or_imprecise_dtypes=True))

    def move(on, out, a, deps):
        return cp(out, a, deps) if on == "v" else act(out, a, F.Copy, deps)

    def quad(t, e, a, b, step=1):
        return t[32 * e:32 * e + 32, a:b:step]

    def order(r):
        c = T.cores[r]
        near = [k for k in range(NR) if topo.chip(T.cores[k]) == topo.chip(c)]
        off = [k for k in range(NR) if k not in near]
        i = near.index(r)
        return [off[1 - i], off[i]] + [k for k in near if k != r] + [r]
    O = order(me)
    come = [O[3], O[0], O[2], O[1]]
    E = sorted((0, 1), key=come.index) + [2, 3]
    B = [E.index(r) for r in O]
    last = B[1]
    late = last < 3
    eoff = topo.engines(core, T.cores[O[0]])
    eon = [e for e in topo.engines(core, T.cores[O[2]]) if e not in eoff] or eoff
    part = {O[0]: eoff, O[1]: eoff, O[2]: eon}

    def mask(es):
        return sum(1 << e for e in es)

    lg = dma("s", "lg", T.gs[:], T.wg[:, 0:16])
    lx = [dma("y", "lx%d" % i, T.xs[:, 4 * a:4 * b], T.x[:, 4 * a:4 * b]) for i, (a, b) in enumerate(XP)]
    need("y", lx)
    lw = dma("y", "lw", T.ws1[:], T.w1[:])
    lsh = {0: lx}
    for t in (2, 1, 3):
        lsh[t] = [dma("y", "lh%d" % t, T["xs%d" % t][:, 16 - t:2064 - t], T.x[:])]

    ip = done("g", g.iota(T.ip[:], [[0, 32]], 0, 1))
    ic = done("g", g.iota(T.ic[:], [[4, 4], [0, 8]], 0, 0))
    on1 = ms(T.ones[:], 1.0)
    ez = ms(T.et[:, 0:1024], 0.0)
    ez = act(T.et[:, 1024:2048], T.et[:, 0:1024], F.Copy, [ez])
    need("g", [on1])
    idn = done("g", g.affine_select(T.idn[:], T.ones[:], [[-1, 128]], A.is_equal, 0.0, 0, 1))
    ms(T.za[:, 16:48], BIG)
    t2 = ts(T.t2[:], T.ip[:], 3, A.bitwise_and, deps=[ip])
    ms(T.zb[:, 16:48], -BIG)
    l1 = tt(T.l1[:], T.ic[:], T.t2[:], A.add, [ic, t2])
    ms(T.cb[:, 0:16], 0.0)
    o1 = cp(T.o1[:], T.l1[:], [l1])
    ms(T.dd[:, 511:512], float(CK))
    ms(T.X0[:], 0.0)
    ms(T.nb[:, 0:1], (NT - 2 * CK + 1) / 32 * BIG)
    ms(T.nb[:, 1:2], (NT - 2 * CK - 0.5) * BIG)
    ms(T.D[:, 0:800:200], 0.0)
    pz = ms(T.P[:, 0:4 * PW:PW], 0.0)
    for e in range(NR):
        iota(quad(T.k2, e, 0, 8), [[64, 8]], 1, 2)
        kb = iota(quad(T.base, e, 0, 8), [[0, 8]], CK * E.index(e), 0)
    g1 = [move("vs"[a], T.gl1[:, 256 * a:256 * a + 256], T.gs[:, 0:16].indirect(T.o1[:, 16 * a:16 * a + 16]), [lg, o1])
          for a in range(2)]
    g1 = quant(T.g1q[:], T.g1c[:], T.gl1[:], g1)
    et = [act(T.et[:, 512 * b + b:512 * b + 512:4], T.idn[:], F.Copy, [ez, idn]) for b in range(4)]

    def xquant(i):
        a, b = XP[i]
        return quant(T.xq[:, a:b], T.xc[:, a:b], T.xs[:, 4 * a:4 * b], [lx[i]])

    def scores(bank, a, b, deps):
        return mm(bank[:, 0:b - a], T.g1q[:], T.g1c[:], T.xq[:, a:b], T.xc[:, a:b], deps)

    def sign(c, k, bank, a, n, deps):
        return act(T.junk[:, 512 * c + a:512 * c + a + n], bank[:, 0:n], F.Sign, deps,
                   bias=T.zT[:, 32 * c:32 * c + 1], scale=-1.0, accum_out=T.accS[:, k:k + 1])

    def above(i, bank, a, n, deps):
        c = NS + i
        return ts(T.cmp[:, 512 * i + a:512 * i + a + n], bank[:, 0:n], T.zT[:, 32 * c:32 * c + 1], A.is_gt, BIG, A.mult, deps)
    h0 = 32 * (8 - EV)
    x0 = xquant(0)
    zA, zA2 = scores(T.ps2, 0, 256, [g1, x0]), scores(T.ps4, 0, 256, [])
    eqd = quant(T.eq[:, 0:256], T.ec[:, 0:256], T.et[:, 0:1024], et[0:2])
    ta = tr(T.zT[:, 0:h0], T.ps2[:, 0:h0], [zA])
    tb = tr(T.zT[:, 32 * NS:32 * (NS + EV)], T.ps2[:, h0:256])
    for c in range(ES):
        sign(c, c, T.ps4, 0, 256, [zA2, ta])
    x1 = xquant(1)
    above(0, T.ps2, 0, 256, [tb])
    x2 = xquant(2)
    zB, zB2 = scores(T.ps3, 256, 512, [x1, x2]), scores(T.ps5, 256, 512, [])
    zS, zV = scores(T.ps1, 0, 512, []), scores(T.ps0, 0, 512, [])
    for i in range(1, EV):
        above(i, T.ps2, 0, 256, [])
    tc = tr(T.zT[:, h0:32 * NS], T.ps3[:, 0:32 * NS - h0], [zB])
    td = tr(T.zT[:, 32 * (NS + EV):512], T.ps3[:, 32 * NS - h0:256])
    for c in range(ES):
        aH = sign(c, NS + c, T.ps5, 256, 256, [zB2])
    for c in range(ES, NS):
        aS = sign(c, c, T.ps1, 0, 512, [zS, tc])
    def wquant(i):
        return quant(T.wq[:, 128 * i:128 * i + 128], T.wc[:, 128 * i:128 * i + 128], T.ws1[:, 512 * i:512 * i + 512], [lw])

    prev, m1 = None, []
    for i in range(NV + 1):
        if i < NV:
            cur = above(i, T.ps3, 256, 256, []) if i < EV else above(i, T.ps0, 0, 512, [zV, td])
        else:
            wquant(0)
        if i > 0:
            k = i - 1
            m1 = [scan(T.mk[:, NS + k + 255:NS + k - 1:-1], T.cmp[:, 512 * k:512 * k + 256],
                       T.cmp[:, 512 * k + 256:512 * k + 512], (0.5 - CK) * BIG, A.add, A.add, [prev] + m1)]
        if i == NV - 2:
            aH = tt(T.accS[:, 0:ES], T.accS[:, 0:ES], T.accS[:, NS:NS + ES], A.add, [aH])
        prev = cur
    m0 = act(T.mk[:, 0:NS], T.accS[:, 0:NS], F.Identity, [aS, aH], scale=-BIG, bias=T.nb[:, 1:2])
    za = tt(T.za[:, 0:16], T.zT[:, 0:512:32], T.mk[:, 0:16], A.max, [m0] + m1)
    zb = tt(T.zb[:, 0:16], T.zT[:, 0:512:32], T.mk[:, 0:16], A.min)
    rn = act(T.sg[:], T.mk[:, 0:16], F.Sign, [m0] + m1, accum_out=T.rn[:])
    xn = act(T.ex[:, 48:80], T.zb[:, 16:48], F.Identity, [rn], scale=T.rn[:], bias=T.nb[:, 0:1])
    xa = scan(T.ex[:, 0:48], T.za[:], T.za[:], BIG, A.min, A.min, [za])
    xb = scan(T.ex[:, 127:79:-1], T.zb[:], T.zb[:], -BIG, A.max, A.max, [zb])
    wquant(1)
    xt = tr(T.exT[:], T.ex[:, 16:112], [xa, xb, xn])
    wquant(2)
    ns = red(T.ns[:], T.exT[:, 32:64], A.add, [xt])
    wq = wquant(3)
    vs = scan(T.vs[:], T.exT[:, 0:32], T.exT[:, 64:96], T.ns[:], A.min, A.max, [ns])
    quant(T.eq[:, 256:384], T.ec[:, 256:384], T.et[:, 1024:1536], et)
    sA = act(T.sgA[:], T.ps1[:], F.Sign, [vs], bias=T.vs[:, 31:32], scale=-1.0)
    gt = ts(T.gt[:], T.ps0[:], T.vs[:, 31:32], A.is_gt, -1.0, A.mult, [vs])
    g0 = act(T.ge[:, 0:GS], T.sgA[:, 0:GS], F.Sign, [sA], bias=1.0, scale=-1.0)
    g1 = ts(T.ge[:, GS:512], T.sgA[:, GS:512], 0.0, A.is_le, deps=[sA])
    dd = scan(T.dd[:, 510::-1], T.gt[:, 511:0:-1], T.gt[:, 511:0:-1], float(CK), A.add, A.max, [gt])
    eqd = quant(T.eq[:, 384:512], T.ec[:, 384:512], T.et[:, 1536:2048])
    C = scan(T.cb[:, 16:528], T.ge[:], T.dd[:], 0.0, A.add, A.min, [dd, g0, g1])
    for c in range(CS):
        aS = act(T.jk2[:, WS * c:WS * c + WS], T.cb[:, 528 - WS:528], F.Sign, [C, kb],
                 bias=T.k2[:, CV + c:CV + c + 1], scale=-2.0, accum_out=T.acc2[:, c:c + 1])
    H = WV // 2
    for i in range(CV + 1):
        if i < CV:
            cur = ts(T.cm2[:, WV * i:WV * i + WV], T.cb[:, 16 + 32 * i:16 + 32 * i + WV], 2.0, A.mult,
                     T.k2[:, i:i + 1], A.is_lt, [C, kb])
        if i > 0:
            k = i - 1
            wV = scan(T.sc2[:, H * k:H * k + H], T.cm2[:, WV * k:WV * k + H], T.cm2[:, WV * k + H:WV * k + WV],
                      32.0 * k - 256.0, A.add, A.add, [prev])
        prev = cur

    def marks():
        for a in range(0, NT, 128):
            tk = tt(T.tk[:, a:a + 128], T.cb[:, 16 + a:144 + a], T.cb[:, 15 + a:143 + a], A.subtract, [C])
            yield tk
        for a in range(0, NT, 128):
            yield tt(T.mr[:, a:a + 128], T.cb[:, 16 + a:144 + a], T.tk[:, a:a + 128], A.mult, [tk])
    mark = marks()
    next(mark)
    x0 = []
    for o in range(NR):
        x0.append(act(T.X0[0:32, 6 * o + CV:6 * o + 6], quad(T.acc2, O[o], 0, CS), F.Identity, [aS, pz],
                      scale=2.0, bias=4.0 * (NT - WS) + 2.0 * WS))
    for o in range(NR):
        out, src = T.X0[0:32, 6 * o:6 * o + CV], quad(T.sc2, O[o], H - 1, H * CV, H)
        x0.append(ts(out, src, 4.0, A.mult, 1024.0, A.add, [wV]) if o % 2 == 0 else
                  act(out, src, F.Identity, [wV], scale=4.0, bias=1024.0))

    def wrap(n, W, Z, z):
        d0 = cp(Z[0:n, 0:16], Z[0:n, 16:32], [z])
        yield d0
        d1 = cp(Z[0:n, 48:64], Z[0:n, 32:48])
        yield d1
        yield tr(W[0:n, 0:64:2], Z[0:n, 0:32], [d0])
        yield tr(W[0:n, 1:64:2], Z[0:n, 32:64], [d1])
    next(mark)
    for a in range(2):
        z = tr(quad(T.Z0, a, 16, 48), T.X0[0:32, 0:32], x0)
    next(mark)
    w = list(wrap(64, T.W0, T.Z0, z))[-1]
    next(mark)
    for a in range(2):
        wr = cp(T.tokw[64 * a:64 * a + 64, :], T.W0[0:64, 0:48], [w])
    mr = [next(mark)]

    def gather(o, on="vvss"):
        r = []
        for t in range(4):
            out = T.h[:, 768 * o + t:768 * o + 768:4]
            win = T.xs[:, 0:2048] if t == 0 else T["xs%d" % t][:, 16:2064 - t]
            r.append(move(on[t], out, win.indirect(T.tokw[:, 12 * o:12 * o + 12]), [wr] + lsh[t]))
        mr[0] = next(mark, mr[0])
        return quant(T.sq[:, CK * o:CK * o + CK], T.sc[:, CK * o:CK * o + CK], T.h[:, 768 * o:768 * o + 768], r)

    def send(o, sb, sp, db, dp, sem, dep):
        r = O[o]
        p = order(r).index(me)
        rid, pid, _ = topo.addr(T.cores[r])
        need("g", [dep])
        for a, b, code in ((sb, db, True), (sp, dp, False)):
            src, dst = T[a][:, CK * o:CK * o + CK], T[b][:, CK * p:CK * p + CK]
            if code:
                src, dst = src.bitcast(dt.uint8), dst.bitcast(dt.uint8)
            g.remote_dma(out_ap=dst, in_ap=src, remote_sem=S["%s%d" % (sem, me)], local_sem=S["sent"], pid=pid,
                         routing_id=rid, dma_engine_mask=mask(part[r]))
            tot["sent"] = tot.get("sent", 0) + len(part[r])

    def arrived(sem, o):
        return (sem + str(O[o]), 2 * len(part[O[o]]))

    for o in DO:
        send(o, "sq", "sc", "rq", "rc", "rd", gather(o))

    free = [[sA, gt], [sA]]
    lst = [None]

    def expert(bset, cq, cc, o, qout, qsc, z, deps, k):
        rd, m = [], {}
        for i in (2, 0, 3, 1):
            m[i] = mm(T["ps%d" % (4 * bset + i)][:, 0:CK], T.wq[:, 128 * i:128 * i + 128], T.wc[:, 128 * i:128 * i + 128],
                      T[cq][:, CK * o:CK * o + CK], T[cc][:, CK * o:CK * o + CK], list(deps) + [wq] + free[bset])
        for i in range(4):
            out = T.rt[:, 768 * o + i:768 * o + 768:4]
            src = T["ps%d" % (4 * bset + i)][:, 0:CK]
            if i < 2:
                rd.append(ts(out, src, 0.0, A.max, 0.05, A.mult, [m[i]]))
                fill(k if i == 0 else 0)
            else:
                rd.append(act(out, src, F.Relu, [m[i]], scale=0.05))
        free[bset] = rd
        return quant(T[qout][:, CK * z:CK * z + CK], T[qsc][:, CK * z:CK * z + CK], T.rt[:, 768 * o:768 * o + 768], rd)

    tr4 = ts(T.tokr[:], T.tokw[:], 0.25, A.mult, deps=[wr])
    qown = gather(3, OG)
    tr(T.mT[:, 0:512], T.mr[:, 0:512], mr)
    for i in range(3):
        c0 = 12 * B.index(3 - i)
        xl = act(T.mr[:, 512 + CK * i:512 + CK * (i + 1)], T.mr[:, 0:512].indirect(T.tokr[:, c0:c0 + 12]), F.Copy, mr + [tr4])

    n = 128 if late else 64

    def lists():
        x = tr(T.mT[:, 512:1088], T.mr[:, 512:1088], [xl])
        yield x
        x = ts(T.pu[:], T.mT[:, 0:1088:32], 1024.0, A.mult, T.base[:, 0:1], A.min, [x])
        yield x
        x = tt(T.pos[:], T.pu[:], T.mT[:, 0:1088:32], A.add, [x])
        yield x
        for q, m in ((1, 28), (2, 22)):
            x = tt(quad(T.pos, E[0], 0, m), quad(T.pos, E[0], 0, m), quad(T.pos, E[q], 0, m), A.max, [x])
            yield x
        yield cp(T.X0[32:64, 32:50], quad(T.pos, E[0], 16, 34), [x])
        if late:
            yield cp(T.X0[64:96, 32:48], quad(T.pos, E[0], 0, 16))
            yield cp(T.X0[96:128, 32:48], quad(T.mT, E[3], 0, 512, 32))
        x = tt(T.X0[0:32, 32:48], quad(T.pos, E[0], 0, 16), quad(T.pos, E[3], 0, 16), A.max)
        yield x
        x = tr(T.Z1[0:n, 16:48], T.X0[0:n, 32:64], [x])
        yield x
        yield from wrap(n, T.W1, T.Z1, x)
    todo = lists()

    def fill(k):
        for _ in range(k):
            lst[0] = next(todo, lst[0])
    fill(F0[0])
    q3 = expert(1, "sq", "sc", 3, "bq", "bc", 3, [qown], F0[1])
    fill(FILL[0])
    for k, (bset, o) in enumerate(zip((0, 1, 0), EO)):
        send(o, "oq", "oc", "bq", "bc", "rr", expert(bset, "rq", "rc", o, "oq", "oc", o, [arrived("rd", o)], FI))
        fill(FILL[k + 1])

    dm, got, gs, sb = {}, {}, {}, {}
    read = {k: free[k // 4] for k in range(8)}

    def decode(o, rows, banks):
        for b, k in zip(rows, banks):
            m = mm(T["ps%d" % k][:, 0:CK], T.eq[:, 128 * b:128 * b + 128], T.ec[:, 128 * b:128 * b + 128],
                   T.bq[:, CK * o:CK * o + CK], T.bc[:, CK * o:CK * o + CK],
                   [q3 if o == 3 else arrived("rr", o), eqd] + read[k])
            dm[(B[o], b)] = (m, k)

    def take(q, b, call):
        m, k = dm[(q, b)]
        read[k] = [call(T["ps%d" % k][:, 0:CK], m)]
        return read[k][0]

    def slots(q, b):
        return T.P[:, PW * b + 1 + CK * q:PW * b + 1 + CK * (q + 1)]

    def earlier(q, b):
        return T.P[:, PW * b:PW * b + 1 + CK * q].indirect(T.oL[:, 68 - 12 * q:80 - 12 * q])

    def first(rows):
        for b in rows:
            got[b] = take(0, b, lambda src, m: move("svsv"[b], slots(0, b), src, [m]))

    def pick(q, rows, on):
        for b in rows:
            out = T.G[:, 768 * (q - 1) + CK * b:768 * (q - 1) + CK * b + CK]
            gs[b] = (move(on[b], out, earlier(q, b), [got[b], oL]), out)

    def add(q, rows):
        for b in rows:
            got[b] = take(q, b, lambda src, m: tt(slots(q, b), src, gs[b][1], A.add, [m, gs[b][0], got[b]]))

    def parked(q, b, a=1):
        c0 = 200 * (2 * (q - 2) + b - 2)
        return T.D[:, c0 + a:c0 + 1 + CK]

    def park(q, rows=FB[::-1]):
        for b in rows:
            sb[(q, b)] = take(q, b, lambda src, m: move("vs"[b - 2], parked(q, b), src, [m]))

    def spread(q):
        if q == 3:
            bytoken(2, 0, 512)
            bytoken(3, 0, 512 if B[3] == 3 else 256)

    def fused(q, b):
        got[b] = tt(slots(q, b), earlier(q, b), parked(q, b), A.add, [got[b], sb[(q, b)]])

    def tokens(b, n, i, a, z):
        return T.P[:, PW * b:PW * b + 1 + n * CK].indirect(T.oL[:, LO[i] + a // 16:LO[i] + z // 16])

    def bytoken(b, a, z):
        src = parked(3, b, 0).indirect(T.oL[:, LO[3] + a // 16:LO[3] + z // 16])
        d3.append((b, a, move("vs"[b - 2], T.D3[:, 512 * (b - 2) + a:512 * (b - 2) + z], src, [sb[(3, b)], oL])))

    rest, d3 = (1, 0), []
    rows = rest + FB
    if last == 1:
        decode(3, rows, (4, 5, 6, 7))
        own = [lambda: first(rest), lambda: first(FB)]
    else:
        decode(3, FB[::-1], (6, 7))
        own = [lambda: park(B[3]), lambda: None]
    fill(1)
    own[0]()
    fill(99)
    own[1]()
    y = [move("vs"[a], quad(T.fL, a, LO[i], LO[i + 1]), quad(T.W1, i, 0, LO[i + 1] - LO[i]), lst)
         for i in range(n // 32) for a in range(2)]
    for a in range(2):
        oL = cp(T.oL[64 * a:64 * a + 64, 0:LO[n // 32]], T.fL[0:64, 0:LO[n // 32]], y)
    if last == 1:
        pick(1, rows, "svsv")
        for o, k in ((0, 0), (2, 4)):
            decode(o, FB[::-1] + rest, range(k, k + 4))
            park(B[o])
            spread(B[o])
        decode(1, rows, (0, 1, 4, 5))
        add(1, rows)
        pick(2, rest, "ss")
        add(2, rest)
        pick(3, rest, "ss")
        bytoken(3, 256, 512)
        for b in FB:
            fused(2, b)
        add(3, rest)
    else:
        spread(B[3])
        decode(0, rows, (0, 1, 2, 3))
        first(rows)
        decode(2, rows, (4, 5, 6, 7))
        pick(1, rows, P1)
        add(1, rows)
        if not late:
            decode(3, rest, (0, 1))
            pick(2, rest, "ss")
            for b, c in zip(FB, rest):
                fused(2, b)
                add(2, [c])
        pick(last, rows if late else FB + rest, P2)
        decode(1, rows, (0, 1, 2, 3) if late else (4, 5, 6, 7))
        add(last, rows if late else FB + rest)
        if late:
            decode(3, rest, (4, 5))
            pick(3, rest, "ss")
            add(3, rest)
    for a, z in YP:
        r = []
        for b in rest + FB:
            out = T.ys[:, 4 * a + b:4 * z:4]
            if late and b in FB:
                r.append(tt(out, tokens(b, 3, 2, a, z), T.D3[:, 512 * (b - 2) + a:512 * (b - 2) + z], A.add,
                            [got[b]] + [d for c, s, d in d3 if c == b and s < z]))
            else:
                r.append(move("ssvv"[b], out, tokens(b, 4, 0, a, z), [got[b], oL]))
        st = dma("y", "sty", T.y[:, 4 * a:4 * z], T.ys[:, 4 * a:4 * z], r)
    need("y", [(k, n) for k, n in tot.items()] + [("c" + k, n) for k, n in cnt.items()])
